import numpy as np
import ml_dtypes


def mxq(x, axis, fmt="e4m3"):
    dtype, down = {"e4m3": (ml_dtypes.float8_e4m3fn, 7), "e5m2": (ml_dtypes.float8_e5m2, 14)}[fmt]
    v = np.moveaxis(np.asarray(x, np.float32).astype(ml_dtypes.bfloat16).astype(np.float64), axis, -1)
    blocks = v.reshape(v.shape[:-1] + (-1, 32))
    amax = np.abs(blocks).max(-1, keepdims=True)
    byte = np.maximum(np.where(amax > 0, np.frexp(amax)[1] - 1 + 127, 0) - down, 1)
    scale = np.exp2(byte - 127.0)
    codes = (blocks / scale).astype(np.float32).astype(dtype).astype(np.float64)
    return np.moveaxis((codes * scale).reshape(v.shape), -1, axis)


WIDE = False


def mx_kscale(k):
    if not WIDE:
        return np.ones(k)
    levels = np.array([10, -10, 5, -5, 0])
    if k % 512:
        return np.exp2(np.random.permutation(np.resize(levels, k // 32))).repeat(32)
    a = np.empty((k // 512, 16))
    for p in range(k // 512):
        a[p, :8] = np.random.permutation(np.resize(levels, 8))
        for g in range(8):
            far = levels[np.abs(levels - a[p, g]) >= 10]
            a[p, g + 8] = far[np.random.randint(len(far))]
    return np.exp2(a.ravel()).repeat(32)


def f64(x):
    return np.asarray(x).astype(np.float64)


def striped(idx):
    return np.tile(idx.reshape(-1, 16).T, (8, 1)).astype(np.uint16)


def unstriped(offs):
    return offs[:16].T.reshape(-1).astype(np.int64)


E2M1 = np.array([0.0, 0.5, 1.0, 1.5, 2.0, 3.0, 4.0, 6.0, -0.0, -0.5, -1.0, -1.5, -2.0, -3.0, -4.0, -6.0])


def pack_weight(w, fmt):
    k, n = w.shape
    w = f64(np.asarray(w, np.float32).astype(ml_dtypes.bfloat16)).reshape(k // 32, 32, n)
    amax = np.abs(w).max(1)
    if fmt == "e4m3":
        byte = np.frexp(amax)[1] - 1 + 127 - 7
    else:
        mant, ex = np.frexp(amax / 6.0)
        byte = np.where(mant > 0.5, ex, ex - 1) + 127
    byte = np.clip(np.where(amax > 0, byte, 1), 1, 254)
    scaled = (w * np.exp2(127.0 - byte)[:, None, :]).reshape(k, n).astype(np.float32)
    by_word = np.ascontiguousarray(scaled.reshape(k // 512, 128, 4, n).transpose(0, 1, 3, 2))
    if fmt == "e4m3":
        words = by_word.astype(ml_dtypes.float8_e4m3fn).view(np.uint8)
    else:
        c = by_word.astype(ml_dtypes.float4_e2m1fn).view(np.uint8) & 0xF
        words = (c[..., 0::2] | (c[..., 1::2] << 4)).reshape(k // 512, 128, 2 * n)
    return np.ascontiguousarray(words), np.ascontiguousarray(byte.astype(np.uint8).reshape(k // 512, 16, n))


def unpack_weight(words, scales, fmt):
    g, _, n = scales.shape
    words = np.ascontiguousarray(words).reshape(g, 128, n, -1)
    if fmt == "e4m3":
        vals = words.view(ml_dtypes.float8_e4m3fn).astype(np.float64)
    else:
        nib = np.empty((g, 128, n, 4), np.uint8)
        nib[..., 0::2] = words & 0xF
        nib[..., 1::2] = words >> 4
        vals = E2M1[nib]
    vals = vals * np.repeat(np.exp2(scales.astype(np.float64) - 127.0), 8, axis=1)[..., None]
    return vals.transpose(0, 1, 3, 2).reshape(g * 512, n)


def gelu(v):
    return 0.5 * v * (1.0 + np.tanh(np.sqrt(2.0 / np.pi) * (v + 0.044715 * v**3)))


K, K2, H, N, T, T2, S = 1024, 512, 512, 256, 4096, 2048, 1024

def setup_inputs():
    n = np.random.standard_normal
    s, s2 = mx_kscale(K)[:, None], mx_kscale(K2)[:, None]
    u = mx_kscale(H)[:, None]
    tab_words, tab_scales = pack_weight(n((K, T)) * s, "e4m3")
    tab2_words, tab2_scales = pack_weight(n((K2, T2)) * s2, "e4m3")
    wv_words, wv_scales = pack_weight(n((K, H)) / np.sqrt(K) / s * u.T, "e2m1")
    return {
        "tab_words": tab_words, "tab_scales": tab_scales,
        "tab2_words": tab2_words, "tab2_scales": tab2_scales,
        "offs": striped(np.random.permutation(T)[:S]),
        "offs2": striped(np.random.permutation(T2)[:S]),
        "wg": (n((K, H)) / np.sqrt(K) / s).astype(np.float32),
        "bg": (0.5 * n(H)).astype(np.float32),
        "wv_words": wv_words, "wv_scales": wv_scales,
        "ws": (n((K2, H)) / np.sqrt(K2) / s2 * u.T).astype(np.float32),
        "wo": (n((H, N)) / np.sqrt(H) / u).astype(np.float32),
        "bo": (0.5 * n(N)).astype(np.float32),
    }

def reference(tab_words, tab_scales, tab2_words, tab2_scales, offs, offs2,
              wg, bg, wv_words, wv_scales, ws, wo, bo):
    v = unpack_weight(tab_words, tab_scales, "e4m3")[:, unstriped(offs)]
    v2 = unpack_weight(tab2_words, tab2_scales, "e4m3")[:, unstriped(offs2)]
    wv = unpack_weight(wv_words, wv_scales, "e2m1")
    a = (mxq(f64(wg), 0, "e4m3").T @ v) + f64(bg)[:, None]
    c = wv.T @ v
    d = mxq(f64(ws), 0, "e4m3").T @ v2
    h = 1.0 / (1.0 + np.exp(-a)) * c + d
    hq = mxq(h, 0, "e4m3")
    return (mxq(f64(wo), 0, "e4m3").T @ hq) + f64(bo)[:, None]

@@ -1,0 +1,294 @@
+from contextlib import ExitStack
+
+import concourse.mybir as mybir
+
+K, K2, H, N, T, T2, S = 1024, 512, 512, 256, 4096, 2048, 1024
+FLOPS = 2 * S * (2 * K * H + K2 * H + H * N)
+
+F32 = mybir.dt.float32
+BF16 = mybir.dt.bfloat16
+I32 = mybir.dt.int32
+U32 = mybir.dt.uint32
+U16 = mybir.dt.uint16
+U8 = mybir.dt.uint8
+FP8X4 = mybir.dt.float8_e4m3fn_x4
+FP4X4 = mybir.dt.float4_e2m1fn_x4
+ACT = mybir.ActivationFunctionType
+ALU = mybir.AluOpType
+
+P = 128
+PACK = 4
+K_PASS = P * PACK
+HALF = 512
+CHUNK = 128
+LIST_COLS = S // 16
+ROAD_ROWS = (16, 112)
+SENSOR_ROWS = 112
+SENSOR_ROW = 4
+OUT_GROUPS = ((0, 512), (512, 256), (768, 256))
+
+
+def tile_list_traffic_gated_forecast_kernel(
+    tc, tab_words, tab_scales, tab2_words, tab2_scales, offs, offs2,
+    wg, bg, wv_words, wv_scales, ws, wo, bo, out,
+):
+    nc = tc.nc
+    with ExitStack() as ctx:
+        keep = ctx.enter_context(tc.tile_pool(name="keep", bufs=1))
+        psum = ctx.enter_context(tc.psum_pool(name="psum", bufs=8))
+
+        def held(name, shape, dtype, slot=""):
+            return keep.tile(shape, dtype, name=name, tag=slot or name, align_bytes=64)
+
+        road_list = keep.tile([P, LIST_COLS], U16, name="road_list")
+        sensor_list = keep.tile([P, LIST_COLS], U16, name="sensor_list")
+        road_words = [held("road_words%d" % a, [P, T], I32) for a in range(2)]
+        sensor_words = held("sensor_words", [P, T2], I32)
+        road_scales = held("road_scales", [P, T // 4], I32)
+        sensor_scales = held("sensor_scales", [P, T2 // 4], I32)
+        wv_raw = held("wv_raw", [P, 2, H // 2], I32)
+        wv_scales_raw = held("wv_scales_raw", [P, 2, H // 4], I32)
+        v_planes = held("v_planes", [P, 2, S // 4], I32)
+        v2_plane = held("v2_plane", [P, S // 4], I32)
+        wv_planes = held("wv_planes", [P, 2, H // 4], I32)
+        wg_raw = [held("wg_raw%d" % a, [P, PACK, H], F32) for a in range(2)]
+        ws_raw = held("ws_raw", [P, PACK, H], F32)
+        wo_raw = held("wo_raw", [P, PACK, N], F32)
+        gate_bias = held("gate_bias", [P, PACK, 8], F32)
+        out_bias = held("out_bias", [P, N // P], F32)
+        warm_in = held("warm_in", [P, 1], F32)
+        warm_out = held("warm_out", [P, 1], F32)
+
+        nc.vector.memset(warm_in[:], 0.0)
+        nc.scalar.activation(warm_out[:], warm_in[:], ACT.Sigmoid)
+        for lo, hi in ((0, 16), (32, 64), (64, 112)):
+            nc.vector.memset(road_scales[lo:hi, :], 0)
+        nc.vector.memset(sensor_scales[0:SENSOR_ROWS, :], 0)
+        nc.vector.memset(v_planes[:], 0)
+        nc.vector.memset(v2_plane[:], 0)
+        nc.vector.memset(wv_planes[:], 0)
+
+        def load_words(tile, words, lo, hi):
+            flat = words.rearrange("p t i -> p (t i)")
+            nc.sync.dma_start(out=tile[:, lo:hi], in_=flat[:, 4 * lo : 4 * hi].bitcast(I32))
+
+        def load_weight(tile, rows):
+            nc.sync.dma_start(out=tile[:], in_=rows.rearrange("(p j) c -> p j c", j=PACK))
+
+        nc.sync.dma_start(road_list[:], offs)
+        for a in range(2):
+            nc.sync.dma_start(
+                out=road_scales[ROAD_ROWS[a] : ROAD_ROWS[a] + 16, :], in_=tab_scales[a].bitcast(I32)
+            )
+        nc.sync.dma_start(sensor_list[:], offs2)
+        nc.sync.dma_start(out=sensor_scales[SENSOR_ROWS:P, :], in_=tab2_scales[0].bitcast(I32))
+        load_weight(wg_raw[0], wg[0:K_PASS, :])
+        load_words(road_words[0], tab_words[0], 0, T)
+        for quad in range(4):
+            nc.sync.dma_start(
+                out=wv_scales_raw[32 * quad : 32 * quad + 4, :, :],
+                in_=wv_scales[:, 4 * quad : 4 * quad + 4, :].rearrange("a r n -> r a n").bitcast(I32),
+            )
+        load_weight(wg_raw[1], wg[K_PASS:K, :])
+        load_words(road_words[1], tab_words[1], 0, T // 2)
+        nc.sync.dma_start(out=wv_raw[:], in_=wv_words.rearrange("a p n -> p a n").bitcast(I32))
+        load_words(road_words[1], tab_words[1], T // 2, T)
+        load_weight(ws_raw, ws)
+        load_words(sensor_words, tab2_words[0], 0, T2)
+        wo_rows = wo.rearrange("(b t q) n -> t b q n", t=PACK, q=8)
+        for t in range(PACK):
+            nc.sync.dma_start(out=wo_raw[:, t, :], in_=wo_rows[t])
+
+        with nc.allow_non_contiguous_dma(reason="one bias value a partition"):
+            bg_slots = bg.rearrange("(b t q) -> t b q", t=PACK, q=8)
+            for t in range(PACK):
+                nc.gpsimd.dma_start(out=gate_bias[:, t, 0:1], in_=bg_slots[t].unsqueeze(2))
+            nc.gpsimd.dma_start(out=out_bias[:], in_=bo.rearrange("(c p) -> p c", p=P))
+
+        def gather(name, window, offsets, count, dtype, slot=""):
+            words = count if dtype == U32 else count // 4
+            picked = held(name, [P, words], I32, slot)
+            nc.vector.tensor_copy(picked[:].bitcast(dtype), window[:].bitcast(dtype).indirect(offsets))
+            return picked
+
+        def cast_permuted(name, raw, slot=""):
+            return held(name, [P, PACK, P, PACK], BF16, slot), raw[:].rearrange(
+                "p j (b t u i) -> p t b u j i", t=PACK, u=4, i=2
+            )
+
+        def cast_slot(grouped, source, t):
+            nc.scalar.copy(
+                out=grouped[:, t].rearrange("p (b u i) j -> p b u j i", u=4, i=2), in_=source[:, t]
+            )
+
+        def quantize(name, grouped, width):
+            codes = held(name + "_codes", [P, width], U32)
+            scales = held(name + "_scales", [P, width], U8)
+            nc.vector.quantize_mx(out=codes[:].bitcast(FP8X4), scales=scales[:], in_=grouped)
+            return codes, scales
+
+        road_picked_scales = gather("road_picked_scales", road_scales, road_list[:], S, U8)
+        for a in range(2):
+            for quad in range(4):
+                first = ROAD_ROWS[a] + 4 * quad
+                nc.gpsimd.dma_start(
+                    out=v_planes[32 * quad : 32 * quad + 4, a, :],
+                    in_=road_picked_scales[first : first + 4, :],
+                )
+        sensor_picked_scales = gather("sensor_picked_scales", sensor_scales, sensor_list[:], S, U8)
+        for quad in range(4):
+            first = SENSOR_ROWS + 4 * quad
+            nc.gpsimd.dma_start(
+                out=v2_plane[32 * quad + SENSOR_ROW : 32 * quad + SENSOR_ROW + 4, :],
+                in_=sensor_picked_scales[first : first + 4, :],
+            )
+
+        wg_q = []
+        v_first = None
+        for a in range(2):
+            grouped, source = cast_permuted("wg_grouped%d" % a, wg_raw[a])
+            for t in range(PACK):
+                cast_slot(grouped, source, t)
+            wg_q.append(quantize("wg%d" % a, grouped[:].rearrange("p t m j -> p (t m j)"), H))
+            if a == 0:
+                v_first = gather("v_first", road_words[0], road_list[:], S, U32)
+
+        wv_codes = held("wv_codes", [P, 2, H // 2], I32)
+        for quad in range(4):
+            rows = slice(32 * quad, 32 * quad + 4)
+            nc.vector.tensor_copy(
+                out=wv_planes[rows].rearrange("p a (t b w) -> p a t b w", t=PACK, w=2),
+                in_=wv_scales_raw[rows].rearrange("p a (b t w) -> p a t b w", t=PACK, w=2),
+            )
+        for a in range(2):
+            nc.vector.tensor_copy(
+                out=wv_codes[:, a, :].rearrange("p (t b w) -> p t b w", t=PACK, w=4),
+                in_=wv_raw[:, a, :].rearrange("p (b t w) -> p t b w", t=PACK, w=4),
+            )
+
+        v_second = []
+
+        def road_operand(a, half):
+            cols = slice(half * HALF, (half + 1) * HALF)
+            codes = v_first[:, cols] if a == 0 else v_second[half][:]
+            return codes.bitcast(FP8X4), v_planes[:, a, :].bitcast(U8)[:, cols]
+
+        def gate_pass(bank, a, half, t):
+            codes, scales = wg_q[a]
+            cols = slice(t * P, (t + 1) * P)
+            rhs, rhs_scale = road_operand(a, half)
+            nc.tensor.matmul_mx(
+                out=bank[:], lhsT=codes[:, cols].bitcast(FP8X4), lhsT_scale=scales[:, cols],
+                rhs=rhs, rhs_scale=rhs_scale, start=(a == 0), stop=(a == 1),
+            )
+
+        def value_pass(bank, a, half, t):
+            rhs, rhs_scale = road_operand(a, half)
+            nc.tensor.matmul_mx(
+                out=bank[:],
+                lhsT=wv_codes[:, a, :].bitcast(U8)[:, 2 * t * P : 2 * (t + 1) * P].bitcast(FP4X4),
+                lhsT_scale=wv_planes[:, a, :].bitcast(U8)[:, t * P : (t + 1) * P],
+                rhs=rhs, rhs_scale=rhs_scale, start=(a == 0), stop=(a == 1),
+            )
+
+        gated = [held("gated%d" % half, [P, PACK, HALF], F32) for half in range(2)]
+
+        def gate_times_value(gate_bank, value_bank, half, t):
+            gate = held("gate%d_%d" % (half, t), [P, HALF], F32)
+            nc.scalar.activation(gate[:], gate_bank[:], ACT.Sigmoid, bias=gate_bias[:, t, 0:1])
+            nc.vector.tensor_tensor(gated[half][:, t, :], value_bank[:], gate[:], ALU.mult)
+
+        gate_banks = [psum.tile([P, HALF], F32, name="bank") for t in range(PACK)]
+        value_banks = [psum.tile([P, HALF], F32, name="bank") for t in range(PACK)]
+        for t in range(PACK):
+            gate_pass(gate_banks[t], 0, 0, t)
+        for t in range(PACK):
+            value_pass(value_banks[t], 0, 0, t)
+
+        half_cols = LIST_COLS // 2
+        for half in range(2):
+            offsets = road_list[:, half * half_cols : (half + 1) * half_cols]
+            v_second.append(gather("v_second%d" % half, road_words[1], offsets, HALF, U32))
+
+        for t in range(PACK):
+            gate_pass(gate_banks[t], 1, 0, t)
+            value_pass(value_banks[t], 1, 0, t)
+            gate_times_value(gate_banks[t], value_banks[t], 0, t)
+
+        v2 = []
+        for half in range(2):
+            offsets = sensor_list[:, half * half_cols : (half + 1) * half_cols]
+            v2.append(gather("v2_%d" % half, sensor_words, offsets, HALF, U32, "gate0_%d" % (2 + half)))
+
+        ws_grouped, ws_source = cast_permuted("ws_grouped", ws_raw, "gate0_1")
+        for t in range(PACK):
+            gate_bank = psum.tile([P, HALF], F32, name="bank")
+            value_bank = psum.tile([P, HALF], F32, name="bank")
+            for a in range(2):
+                gate_pass(gate_bank, a, 1, t)
+            for a in range(2):
+                value_pass(value_bank, a, 1, t)
+            gate_times_value(gate_bank, value_bank, 1, t)
+            cast_slot(ws_grouped, ws_source, t)
+        ws_codes, ws_scales = quantize("ws", ws_grouped[:].rearrange("p t m j -> p (t m j)"), H)
+
+        wo_grouped = held("wo_grouped", [P, N, PACK], BF16, "gate1_0")
+        nc.scalar.copy(
+            out=wo_grouped[:].rearrange("p (c i) t -> p c t i", i=2),
+            in_=wo_raw[:].rearrange("p t (c i) -> p c t i", i=2),
+        )
+
+        def add_sensor_part(h_grouped, start, first):
+            half, inside = divmod(start, HALF)
+            bank = psum.tile([P, PACK, CHUNK], F32, name="bank")
+            for t in range(PACK):
+                cols = slice(t * P, (t + 1) * P)
+                nc.tensor.matmul_mx(
+                    out=bank[:, t, :], lhsT=ws_codes[:, cols].bitcast(FP8X4),
+                    lhsT_scale=ws_scales[:, cols],
+                    rhs=v2[half][:, inside : inside + CHUNK].bitcast(FP8X4),
+                    rhs_scale=v2_plane[:].bitcast(U8)[SENSOR_ROW:P, start : start + CHUNK],
+                    start=True, stop=True,
+                )
+            nc.vector.tensor_tensor(
+                h_grouped[:, start - first : start - first + CHUNK, :].rearrange("p (c i) t -> p c t i", i=2),
+                bank[:].rearrange("p t (c i) -> p c t i", i=2),
+                gated[half][:, :, inside : inside + CHUNK].rearrange("p t (c i) -> p c t i", i=2),
+                ALU.add,
+            )
+
+        out_rows = out.rearrange("(c p) j -> p c j", p=P)
+        wo_q = []
+
+        def forecast(h_grouped, first, width, last):
+            codes, scales = quantize("h%d" % first, h_grouped[:].rearrange("p j t -> p (j t)"), width)
+            result = held("result%d" % first, [P, N // P, width], F32)
+            for c in range(N // P):
+                cols = slice(c * P, (c + 1) * P)
+                bank = psum.tile([P, width], F32, name="bank")
+                nc.tensor.matmul_mx(
+                    out=bank[:], lhsT=wo_q[0][:, cols].bitcast(FP8X4), lhsT_scale=wo_q[1][:, cols],
+                    rhs=codes[:].bitcast(FP8X4), rhs_scale=scales[:], start=True, stop=True,
+                )
+                if last and c == 1:
+                    nc.vector.tensor_scalar(
+                        result[:, c, :], bank[:], out_bias[:, c : c + 1], None, ALU.add
+                    )
+                else:
+                    nc.scalar.activation(
+                        result[:, c, :], bank[:], ACT.Identity, bias=out_bias[:, c : c + 1]
+                    )
+            nc.sync.dma_start(out=out_rows[:, :, first : first + width], in_=result[:])
+
+        pending = None
+        for first, width in OUT_GROUPS:
+            h_grouped = held("h_grouped%d" % first, [P, width, PACK], BF16)
+            for start in range(first, first + width, CHUNK):
+                add_sensor_part(h_grouped, start, first)
+                if start == 0:
+                    wo_q.extend(quantize("wo", wo_grouped[:].rearrange("p n t -> p (n t)"), N))
+                if pending is not None:
+                    forecast(*pending)
+                    pending = None
+            pending = (h_grouped, first, width, first + width == S)
+        forecast(*pending)

@@ -1,6 +1,7 @@
 from contextlib import ExitStack
 
 import concourse.mybir as mybir
+from concourse.masks import make_identity
 
 K, K2, H, N, T, T2, S = 1024, 512, 512, 256, 4096, 2048, 1024
 FLOPS = 2 * S * (2 * K * H + K2 * H + H * N)
@@ -21,11 +22,12 @@ PACK = 4
 K_PASS = P * PACK
 HALF = 512
 CHUNK = 128
-LIST_COLS = S // 16
-ROAD_ROWS = (16, 112)
-SENSOR_ROWS = 112
-SENSOR_ROW = 4
 OUT_GROUPS = ((0, 512), (512, 256), (768, 256))
+LIST_COLS = S // 16
+SENSOR_ROW = 8
+SECOND_ROW = 16
+PLANE_ROWS = 100
+BIAS_ROW = 122
 
 
 def tile_list_traffic_gated_forecast_kernel(
@@ -42,68 +44,67 @@ def tile_list_traffic_gated_forecast_kernel(
 
         road_list = keep.tile([P, LIST_COLS], U16, name="road_list")
         sensor_list = keep.tile([P, LIST_COLS], U16, name="sensor_list")
-        road_words = [held("road_words%d" % a, [P, T], I32) for a in range(2)]
-        sensor_words = held("sensor_words", [P, T2], I32)
         road_scales = held("road_scales", [P, T // 4], I32)
         sensor_scales = held("sensor_scales", [P, T2 // 4], I32)
-        wv_raw = held("wv_raw", [P, 2, H // 2], I32)
-        wv_scales_raw = held("wv_scales_raw", [P, 2, H // 4], I32)
-        v_planes = held("v_planes", [P, 2, S // 4], I32)
-        v2_plane = held("v2_plane", [P, S // 4], I32)
         wv_planes = held("wv_planes", [P, 2, H // 4], I32)
-        wg_raw = [held("wg_raw%d" % a, [P, PACK, H], F32) for a in range(2)]
-        ws_raw = held("ws_raw", [P, PACK, H], F32)
-        wo_raw = held("wo_raw", [P, PACK, N], F32)
-        gate_bias = held("gate_bias", [P, PACK, 8], F32)
-        out_bias = held("out_bias", [P, N // P], F32)
+        second_plane = held("second_plane", [P, S // 4], I32)
+        bias_rows = held("bias_rows", [P, P], F32)
+        identity = held("identity", [P, P], F32)
+        bias = held("bias", [P, P - BIAS_ROW], F32)
         warm_in = held("warm_in", [P, 1], F32)
         warm_out = held("warm_out", [P, 1], F32)
 
+        nc.vector.memset(road_scales[:], 0)
         nc.vector.memset(warm_in[:], 0.0)
         nc.scalar.activation(warm_out[:], warm_in[:], ACT.Sigmoid)
-        for lo, hi in ((0, 16), (32, 64), (64, 112)):
-            nc.vector.memset(road_scales[lo:hi, :], 0)
-        nc.vector.memset(sensor_scales[0:SENSOR_ROWS, :], 0)
-        nc.vector.memset(v_planes[:], 0)
-        nc.vector.memset(v2_plane[:], 0)
+        nc.vector.memset(bias_rows[0:BIAS_ROW, :], 0.0)
         nc.vector.memset(wv_planes[:], 0)
+        nc.vector.memset(second_plane[96:P, :], 0)
+        nc.gpsimd.memset(sensor_scales[:], 0)
+        make_identity(nc, identity[:])
 
-        def load_words(tile, words, lo, hi):
-            flat = words.rearrange("p t i -> p (t i)")
-            nc.sync.dma_start(out=tile[:, lo:hi], in_=flat[:, 4 * lo : 4 * hi].bitcast(I32))
+        def load_words(name, words, columns, slot):
+            tile = held(name, [P, columns], I32, slot)
+            nc.sync.dma_start(out=tile[:], in_=words.rearrange("p t i -> p (t i)").bitcast(I32))
+            return tile
 
-        def load_weight(tile, rows):
+        def load_weight(name, rows, slot=""):
+            tile = held(name, [P, PACK, H], F32, slot)
             nc.sync.dma_start(out=tile[:], in_=rows.rearrange("(p j) c -> p j c", j=PACK))
+            return tile
 
         nc.sync.dma_start(road_list[:], offs)
-        for a in range(2):
-            nc.sync.dma_start(
-                out=road_scales[ROAD_ROWS[a] : ROAD_ROWS[a] + 16, :], in_=tab_scales[a].bitcast(I32)
-            )
         nc.sync.dma_start(sensor_list[:], offs2)
-        nc.sync.dma_start(out=sensor_scales[SENSOR_ROWS:P, :], in_=tab2_scales[0].bitcast(I32))
-        load_weight(wg_raw[0], wg[0:K_PASS, :])
-        load_words(road_words[0], tab_words[0], 0, T)
+        nc.sync.dma_start(
+            out=bias_rows[BIAS_ROW : BIAS_ROW + PACK, :],
+            in_=bg.rearrange("(b t q) -> t b q", t=PACK, q=8),
+        )
+        nc.sync.dma_start(out=bias_rows[BIAS_ROW + PACK : P, :], in_=bo.rearrange("(c p) -> c p", p=P))
+        wg_first = load_weight("wg_first", wg[0:K_PASS, :])
+        scale_rows = tab_scales.rearrange("a (quad r) t -> r quad a t", r=4)
+        for r in range(4):
+            nc.sync.dma_start(out=road_scales[r:P:SECOND_ROW, :], in_=scale_rows[r].bitcast(I32))
+        road_first = load_words("road_first", tab_words[0], T, "warm_in")
+        wv_scales_raw = held("wv_scales_raw", [P, 2, H // 4], I32, "warm_out")
         for quad in range(4):
             nc.sync.dma_start(
                 out=wv_scales_raw[32 * quad : 32 * quad + 4, :, :],
                 in_=wv_scales[:, 4 * quad : 4 * quad + 4, :].rearrange("a r n -> r a n").bitcast(I32),
             )
-        load_weight(wg_raw[1], wg[K_PASS:K, :])
-        load_words(road_words[1], tab_words[1], 0, T // 2)
-        nc.sync.dma_start(out=wv_raw[:], in_=wv_words.rearrange("a p n -> p a n").bitcast(I32))
-        load_words(road_words[1], tab_words[1], T // 2, T)
-        load_weight(ws_raw, ws)
-        load_words(sensor_words, tab2_words[0], 0, T2)
-        wo_rows = wo.rearrange("(b t q) n -> t b q n", t=PACK, q=8)
-        for t in range(PACK):
-            nc.sync.dma_start(out=wo_raw[:, t, :], in_=wo_rows[t])
+        for quad in range(4):
+            first = 32 * quad + SENSOR_ROW
+            nc.gpsimd.dma_start(
+                out=sensor_scales[first : first + 4, :],
+                in_=tab2_scales[0, 4 * quad : 4 * quad + 4, :].bitcast(I32),
+            )
 
-        with nc.allow_non_contiguous_dma(reason="one bias value a partition"):
-            bg_slots = bg.rearrange("(b t q) -> t b q", t=PACK, q=8)
-            for t in range(PACK):
-                nc.gpsimd.dma_start(out=gate_bias[:, t, 0:1], in_=bg_slots[t].unsqueeze(2))
-            nc.gpsimd.dma_start(out=out_bias[:], in_=bo.rearrange("(c p) -> p c", p=P))
+        bias_bank = psum.tile([P, P], F32, name="bank")
+        nc.tensor.transpose(bias_bank[:], bias_rows[:], identity[:])
+        nc.scalar.copy(out=bias[:], in_=bias_bank[:, BIAS_ROW:P])
+
+        wg_second = load_weight("wg_second", wg[K_PASS:K, :], "bias_rows")
+        wv_raw = held("wv_raw", [P, 2, H // 2], I32, "identity")
+        nc.sync.dma_start(out=wv_raw[:], in_=wv_words.rearrange("a p n -> p a n").bitcast(I32))
 
         def gather(name, window, offsets, count, dtype, slot=""):
             words = count if dtype == U32 else count // 4
@@ -111,55 +112,44 @@ def tile_list_traffic_gated_forecast_kernel(
             nc.vector.tensor_copy(picked[:].bitcast(dtype), window[:].bitcast(dtype).indirect(offsets))
             return picked
 
-        def cast_permuted(name, raw, slot=""):
-            return held(name, [P, PACK, P, PACK], BF16, slot), raw[:].rearrange(
-                "p j (b t u i) -> p t b u j i", t=PACK, u=4, i=2
-            )
-
-        def cast_slot(grouped, source, t):
-            nc.scalar.copy(
-                out=grouped[:, t].rearrange("p (b u i) j -> p b u j i", u=4, i=2), in_=source[:, t]
-            )
-
-        def quantize(name, grouped, width):
-            codes = held(name + "_codes", [P, width], U32)
+        def quantize(name, grouped, width, slot=""):
+            codes = held(name + "_codes", [P, width], U32, slot)
             scales = held(name + "_scales", [P, width], U8)
             nc.vector.quantize_mx(out=codes[:].bitcast(FP8X4), scales=scales[:], in_=grouped)
             return codes, scales
 
-        road_picked_scales = gather("road_picked_scales", road_scales, road_list[:], S, U8)
-        for a in range(2):
-            for quad in range(4):
-                first = ROAD_ROWS[a] + 4 * quad
-                nc.gpsimd.dma_start(
-                    out=v_planes[32 * quad : 32 * quad + 4, a, :],
-                    in_=road_picked_scales[first : first + 4, :],
-                )
-        sensor_picked_scales = gather("sensor_picked_scales", sensor_scales, sensor_list[:], S, U8)
-        for quad in range(4):
-            first = SENSOR_ROWS + 4 * quad
-            nc.gpsimd.dma_start(
-                out=v2_plane[32 * quad + SENSOR_ROW : 32 * quad + SENSOR_ROW + 4, :],
-                in_=sensor_picked_scales[first : first + 4, :],
+        def cast_slot(grouped, raw, t):
+            source = raw[:].rearrange("p j (b t u i) -> p t b u j i", t=PACK, u=4, i=2)
+            nc.scalar.copy(
+                out=grouped[:, t].rearrange("p (b u i) j -> p b u j i", u=4, i=2), in_=source[:, t]
             )
 
-        wg_q = []
-        v_first = None
-        for a in range(2):
-            grouped, source = cast_permuted("wg_grouped%d" % a, wg_raw[a])
+        def quantize_permuted(name, raw, slot=""):
+            grouped = held(name + "_grouped", [P, PACK, P, PACK], BF16)
             for t in range(PACK):
-                cast_slot(grouped, source, t)
-            wg_q.append(quantize("wg%d" % a, grouped[:].rearrange("p t m j -> p (t m j)"), H))
-            if a == 0:
-                v_first = gather("v_first", road_words[0], road_list[:], S, U32)
+                cast_slot(grouped, raw, t)
+            return quantize(name, grouped[:].rearrange("p t m j -> p (t m j)"), H, slot)
 
-        wv_codes = held("wv_codes", [P, 2, H // 2], I32)
+        wg_q = [quantize_permuted("wg0", wg_first)]
+        road_second = load_words("road_second", tab_words[1], T, "wg_first")
+        packed_planes = gather("packed_planes", road_scales, road_list[:], S, U8)
+        nc.gpsimd.dma_start(
+            out=second_plane[0:PLANE_ROWS, :], in_=packed_planes[SECOND_ROW : SECOND_ROW + PLANE_ROWS, :]
+        )
+        v_first = gather("v_first", road_first, road_list[:], S, U32, "road_scales")
         for quad in range(4):
             rows = slice(32 * quad, 32 * quad + 4)
             nc.vector.tensor_copy(
                 out=wv_planes[rows].rearrange("p a (t b w) -> p a t b w", t=PACK, w=2),
                 in_=wv_scales_raw[rows].rearrange("p a (b t w) -> p a t b w", t=PACK, w=2),
             )
+        v2_plane = gather("v2_plane", sensor_scales, sensor_list[:], S, U8)
+        wg_q.append(quantize_permuted("wg1", wg_second, "sensor_scales"))
+
+        sensor_words = load_words("sensor_words", tab2_words[0], T2, "warm_in")
+        ws_raw = load_weight("ws_raw", ws, "bias_rows")
+
+        wv_codes = held("wv_codes", [P, 2, H // 2], I32, "wg1_grouped")
         for a in range(2):
             nc.vector.tensor_copy(
                 out=wv_codes[:, a, :].rearrange("p (t b w) -> p t b w", t=PACK, w=4),
@@ -170,8 +160,9 @@ def tile_list_traffic_gated_forecast_kernel(
 
         def road_operand(a, half):
             cols = slice(half * HALF, (half + 1) * HALF)
-            codes = v_first[:, cols] if a == 0 else v_second[half][:]
-            return codes.bitcast(FP8X4), v_planes[:, a, :].bitcast(U8)[:, cols]
+            if a == 0:
+                return v_first[:, cols].bitcast(FP8X4), packed_planes[:].bitcast(U8)[:, cols]
+            return v_second[half][:].bitcast(FP8X4), second_plane[:].bitcast(U8)[:, cols]
 
         def gate_pass(bank, a, half, t):
             codes, scales = wg_q[a]
@@ -191,12 +182,10 @@ def tile_list_traffic_gated_forecast_kernel(
                 rhs=rhs, rhs_scale=rhs_scale, start=(a == 0), stop=(a == 1),
             )
 
-        gated = [held("gated%d" % half, [P, PACK, HALF], F32) for half in range(2)]
-
-        def gate_times_value(gate_bank, value_bank, half, t):
-            gate = held("gate%d_%d" % (half, t), [P, HALF], F32)
-            nc.scalar.activation(gate[:], gate_bank[:], ACT.Sigmoid, bias=gate_bias[:, t, 0:1])
-            nc.vector.tensor_tensor(gated[half][:, t, :], value_bank[:], gate[:], ALU.mult)
+        def gate_times_value(gate_bank, value_bank, gated, name, t, slot=""):
+            gate = held(name, [P, HALF], F32, slot)
+            nc.scalar.activation(gate[:], gate_bank[:], ACT.Sigmoid, bias=bias[:, t : t + 1])
+            nc.vector.tensor_tensor(gated[:, t, :], value_bank[:], gate[:], ALU.mult)
 
         gate_banks = [psum.tile([P, HALF], F32, name="bank") for t in range(PACK)]
         value_banks = [psum.tile([P, HALF], F32, name="bank") for t in range(PACK)]
@@ -208,19 +197,30 @@ def tile_list_traffic_gated_forecast_kernel(
         half_cols = LIST_COLS // 2
         for half in range(2):
             offsets = road_list[:, half * half_cols : (half + 1) * half_cols]
-            v_second.append(gather("v_second%d" % half, road_words[1], offsets, HALF, U32))
+            slot = "identity" if half == 0 else ""
+            v_second.append(gather("v_second%d" % half, road_second, offsets, HALF, U32, slot))
 
+        wo_raw = held("wo_raw", [P, PACK, N], F32, "wg_first")
+        wo_rows = wo.rearrange("(b t q) n -> t b q n", t=PACK, q=8)
+        for t in range(PACK):
+            nc.sync.dma_start(out=wo_raw[:, t, :], in_=wo_rows[t])
+
+        gated = [held("gated0", [P, PACK, HALF], F32)]
         for t in range(PACK):
             gate_pass(gate_banks[t], 1, 0, t)
             value_pass(value_banks[t], 1, 0, t)
-            gate_times_value(gate_banks[t], value_banks[t], 0, t)
+            gate_times_value(gate_banks[t], value_banks[t], gated[0], "gate0_%d" % t, t)
 
         v2 = []
         for half in range(2):
             offsets = sensor_list[:, half * half_cols : (half + 1) * half_cols]
             v2.append(gather("v2_%d" % half, sensor_words, offsets, HALF, U32, "gate0_%d" % (2 + half)))
 
-        ws_grouped, ws_source = cast_permuted("ws_grouped", ws_raw, "gate0_1")
+        gated.append(held("gated1", [P, PACK, HALF], F32, "warm_in"))
+        ws_grouped = held("ws_grouped", [P, PACK, P, PACK], BF16, "gate0_1")
+        for t in range(PACK):
+            cast_slot(ws_grouped, ws_raw, t)
+        gate_slots = ("", "", "bias_rows", "gate0_1")
         for t in range(PACK):
             gate_bank = psum.tile([P, HALF], F32, name="bank")
             value_bank = psum.tile([P, HALF], F32, name="bank")
@@ -228,17 +228,18 @@ def tile_list_traffic_gated_forecast_kernel(
                 gate_pass(gate_bank, a, 1, t)
             for a in range(2):
                 value_pass(value_bank, a, 1, t)
-            gate_times_value(gate_bank, value_bank, 1, t)
-            cast_slot(ws_grouped, ws_source, t)
-        ws_codes, ws_scales = quantize("ws", ws_grouped[:].rearrange("p t m j -> p (t m j)"), H)
+            if t == PACK - 1:
+                ws_codes, ws_scales = quantize("ws", ws_grouped[:].rearrange("p t m j -> p (t m j)"), H)
+            gate_times_value(gate_bank, value_bank, gated[1], "gate1_%d" % t, t, gate_slots[t])
 
-        wo_grouped = held("wo_grouped", [P, N, PACK], BF16, "gate1_0")
+        wo_grouped = held("wo_grouped", [P, N, PACK], BF16, "bias_rows")
         nc.scalar.copy(
             out=wo_grouped[:].rearrange("p (c i) t -> p c t i", i=2),
             in_=wo_raw[:].rearrange("p t (c i) -> p c t i", i=2),
         )
 
-        def add_sensor_part(h_grouped, start, first):
+        sensor_banks = {}
+        for start in range(0, S, CHUNK):
             half, inside = divmod(start, HALF)
             bank = psum.tile([P, PACK, CHUNK], F32, name="bank")
             for t in range(PACK):
@@ -250,15 +251,18 @@ def tile_list_traffic_gated_forecast_kernel(
                     rhs_scale=v2_plane[:].bitcast(U8)[SENSOR_ROW:P, start : start + CHUNK],
                     start=True, stop=True,
                 )
+            sensor_banks[start] = bank
+
+        def add_sensor_part(h_grouped, start, first):
+            half, inside = divmod(start, HALF)
             nc.vector.tensor_tensor(
                 h_grouped[:, start - first : start - first + CHUNK, :].rearrange("p (c i) t -> p c t i", i=2),
-                bank[:].rearrange("p t (c i) -> p c t i", i=2),
+                sensor_banks[start][:].rearrange("p t (c i) -> p c t i", i=2),
                 gated[half][:, :, inside : inside + CHUNK].rearrange("p t (c i) -> p c t i", i=2),
                 ALU.add,
             )
 
         out_rows = out.rearrange("(c p) j -> p c j", p=P)
-        wo_q = []
 
         def forecast(h_grouped, first, width, last):
             codes, scales = quantize("h%d" % first, h_grouped[:].rearrange("p j t -> p (j t)"), width)
@@ -267,16 +271,16 @@ def tile_list_traffic_gated_forecast_kernel(
                 cols = slice(c * P, (c + 1) * P)
                 bank = psum.tile([P, width], F32, name="bank")
                 nc.tensor.matmul_mx(
-                    out=bank[:], lhsT=wo_q[0][:, cols].bitcast(FP8X4), lhsT_scale=wo_q[1][:, cols],
+                    out=bank[:], lhsT=wo_codes[:, cols].bitcast(FP8X4), lhsT_scale=wo_scales[:, cols],
                     rhs=codes[:].bitcast(FP8X4), rhs_scale=scales[:], start=True, stop=True,
                 )
                 if last and c == 1:
                     nc.vector.tensor_scalar(
-                        result[:, c, :], bank[:], out_bias[:, c : c + 1], None, ALU.add
+                        result[:, c, :], bank[:], bias[:, PACK + c : PACK + c + 1], None, ALU.add
                     )
                 else:
                     nc.scalar.activation(
-                        result[:, c, :], bank[:], ACT.Identity, bias=out_bias[:, c : c + 1]
+                        result[:, c, :], bank[:], ACT.Identity, bias=bias[:, PACK + c : PACK + c + 1]
                     )
             nc.sync.dma_start(out=out_rows[:, :, first : first + width], in_=result[:])
 
@@ -285,8 +289,8 @@ def tile_list_traffic_gated_forecast_kernel(
             h_grouped = held("h_grouped%d" % first, [P, width, PACK], BF16)
             for start in range(first, first + width, CHUNK):
                 add_sensor_part(h_grouped, start, first)
-                if start == 0:
-                    wo_q.extend(quantize("wo", wo_grouped[:].rearrange("p n t -> p (n t)"), N))
+                if start == CHUNK:
+                    wo_codes, wo_scales = quantize("wo", wo_grouped[:].rearrange("p n t -> p (n t)"), N)
                 if pending is not None:
                     forecast(*pending)
                     pending = None

@@ -22,7 +22,7 @@ PACK = 4
 K_PASS = P * PACK
 HALF = 512
 CHUNK = 128
-OUT_GROUPS = ((0, 512), (512, 256), (768, 256))
+OUT_GROUPS = ((0, 512), (512, 256), (768, 128), (896, 128))
 LIST_COLS = S // 16
 SENSOR_ROW = 8
 SECOND_ROW = 16
@@ -133,7 +133,7 @@ def tile_list_traffic_gated_forecast_kernel(
         wg_q = [quantize_permuted("wg0", wg_first)]
         road_second = load_words("road_second", tab_words[1], T, "wg_first")
         packed_planes = gather("packed_planes", road_scales, road_list[:], S, U8)
-        nc.gpsimd.dma_start(
+        nc.scalar.dma_start(
             out=second_plane[0:PLANE_ROWS, :], in_=packed_planes[SECOND_ROW : SECOND_ROW + PLANE_ROWS, :]
         )
         v_first = gather("v_first", road_first, road_list[:], S, U32, "road_scales")
@@ -143,11 +143,11 @@ def tile_list_traffic_gated_forecast_kernel(
                 out=wv_planes[rows].rearrange("p a (t b w) -> p a t b w", t=PACK, w=2),
                 in_=wv_scales_raw[rows].rearrange("p a (b t w) -> p a t b w", t=PACK, w=2),
             )
-        v2_plane = gather("v2_plane", sensor_scales, sensor_list[:], S, U8)
-        wg_q.append(quantize_permuted("wg1", wg_second, "sensor_scales"))
+        v2_plane = gather("v2_plane", sensor_scales, sensor_list[:], S, U8, "warm_in")
+        wg_q.append(quantize_permuted("wg1", wg_second))
 
-        sensor_words = load_words("sensor_words", tab2_words[0], T2, "warm_in")
         ws_raw = load_weight("ws_raw", ws, "bias_rows")
+        sensor_words = load_words("sensor_words", tab2_words[0], T2, "sensor_scales")
 
         wv_codes = held("wv_codes", [P, 2, H // 2], I32, "wg1_grouped")
         for a in range(2):
@@ -216,7 +216,7 @@ def tile_list_traffic_gated_forecast_kernel(
             offsets = sensor_list[:, half * half_cols : (half + 1) * half_cols]
             v2.append(gather("v2_%d" % half, sensor_words, offsets, HALF, U32, "gate0_%d" % (2 + half)))
 
-        gated.append(held("gated1", [P, PACK, HALF], F32, "warm_in"))
+        gated.append(held("gated1", [P, PACK, HALF], F32, "sensor_scales"))
         ws_grouped = held("ws_grouped", [P, PACK, P, PACK], BF16, "gate0_1")
         for t in range(PACK):
             cast_slot(ws_grouped, ws_raw, t)

@@ -23,6 +23,7 @@ K_PASS = P * PACK
 HALF = 512
 CHUNK = 128
 OUT_GROUPS = ((0, 512), (512, 256), (768, 128), (896, 128))
+POOL_CHUNKS = 1
 LIST_COLS = S // 16
 SENSOR_ROW = 8
 SECOND_ROW = 16
@@ -61,7 +62,6 @@ def tile_list_traffic_gated_forecast_kernel(
         nc.vector.memset(wv_planes[:], 0)
         nc.vector.memset(second_plane[96:P, :], 0)
         nc.gpsimd.memset(sensor_scales[:], 0)
-        make_identity(nc, identity[:])
 
         def load_words(name, words, columns, slot):
             tile = held(name, [P, columns], I32, slot)
@@ -98,6 +98,7 @@ def tile_list_traffic_gated_forecast_kernel(
                 in_=tab2_scales[0, 4 * quad : 4 * quad + 4, :].bitcast(I32),
             )
 
+        make_identity(nc, identity[:])
         bias_bank = psum.tile([P, P], F32, name="bank")
         nc.tensor.transpose(bias_bank[:], bias_rows[:], identity[:])
         nc.scalar.copy(out=bias[:], in_=bias_bank[:, BIAS_ROW:P])
@@ -118,19 +119,19 @@ def tile_list_traffic_gated_forecast_kernel(
             nc.vector.quantize_mx(out=codes[:].bitcast(FP8X4), scales=scales[:], in_=grouped)
             return codes, scales
 
-        def cast_slot(grouped, raw, t):
+        def cast_permuted(name, raw, slot=""):
+            grouped = held(name, [P, PACK, P, PACK], BF16, slot)
             source = raw[:].rearrange("p j (b t u i) -> p t b u j i", t=PACK, u=4, i=2)
-            nc.scalar.copy(
-                out=grouped[:, t].rearrange("p (b u i) j -> p b u j i", u=4, i=2), in_=source[:, t]
-            )
-
-        def quantize_permuted(name, raw, slot=""):
-            grouped = held(name + "_grouped", [P, PACK, P, PACK], BF16)
             for t in range(PACK):
-                cast_slot(grouped, raw, t)
-            return quantize(name, grouped[:].rearrange("p t m j -> p (t m j)"), H, slot)
+                nc.scalar.copy(
+                    out=grouped[:, t].rearrange("p (b u i) j -> p b u j i", u=4, i=2), in_=source[:, t]
+                )
+            return grouped
 
-        wg_q = [quantize_permuted("wg0", wg_first)]
+        def quantize_slots(name, grouped):
+            return quantize(name, grouped[:].rearrange("p t m j -> p (t m j)"), H)
+
+        wg_q = [quantize_slots("wg0", cast_permuted("wg0_grouped", wg_first))]
         road_second = load_words("road_second", tab_words[1], T, "wg_first")
         packed_planes = gather("packed_planes", road_scales, road_list[:], S, U8)
         nc.scalar.dma_start(
@@ -144,17 +145,16 @@ def tile_list_traffic_gated_forecast_kernel(
                 in_=wv_scales_raw[rows].rearrange("p a (b t w) -> p a t b w", t=PACK, w=2),
             )
         v2_plane = gather("v2_plane", sensor_scales, sensor_list[:], S, U8, "warm_in")
-        wg_q.append(quantize_permuted("wg1", wg_second))
-
-        ws_raw = load_weight("ws_raw", ws, "bias_rows")
-        sensor_words = load_words("sensor_words", tab2_words[0], T2, "sensor_scales")
-
-        wv_codes = held("wv_codes", [P, 2, H // 2], I32, "wg1_grouped")
+        wv_codes = held("wv_codes", [P, 2, H // 2], I32, "sensor_scales")
         for a in range(2):
             nc.vector.tensor_copy(
                 out=wv_codes[:, a, :].rearrange("p (t b w) -> p t b w", t=PACK, w=4),
                 in_=wv_raw[:, a, :].rearrange("p (b t w) -> p t b w", t=PACK, w=4),
             )
+
+        wg_q.append(quantize_slots("wg1", cast_permuted("wg1_grouped", wg_second)))
+        ws_raw = load_weight("ws_raw", ws, "bias_rows")
+        sensor_words = load_words("sensor_words", tab2_words[0], T2, "identity")
 
         v_second = []
 
@@ -197,7 +197,7 @@ def tile_list_traffic_gated_forecast_kernel(
         half_cols = LIST_COLS // 2
         for half in range(2):
             offsets = road_list[:, half * half_cols : (half + 1) * half_cols]
-            slot = "identity" if half == 0 else ""
+            slot = "wg1_grouped" if half == 0 else ""
             v_second.append(gather("v_second%d" % half, road_second, offsets, HALF, U32, slot))
 
         wo_raw = held("wo_raw", [P, PACK, N], F32, "wg_first")
@@ -216,10 +216,8 @@ def tile_list_traffic_gated_forecast_kernel(
             offsets = sensor_list[:, half * half_cols : (half + 1) * half_cols]
             v2.append(gather("v2_%d" % half, sensor_words, offsets, HALF, U32, "gate0_%d" % (2 + half)))
 
-        gated.append(held("gated1", [P, PACK, HALF], F32, "sensor_scales"))
-        ws_grouped = held("ws_grouped", [P, PACK, P, PACK], BF16, "gate0_1")
-        for t in range(PACK):
-            cast_slot(ws_grouped, ws_raw, t)
+        gated.append(held("gated1", [P, PACK, HALF], F32, "identity"))
+        ws_grouped = cast_permuted("ws_grouped", ws_raw, "gate0_1")
         gate_slots = ("", "", "bias_rows", "gate0_1")
         for t in range(PACK):
             gate_bank = psum.tile([P, HALF], F32, name="bank")
@@ -229,14 +227,8 @@ def tile_list_traffic_gated_forecast_kernel(
             for a in range(2):
                 value_pass(value_bank, a, 1, t)
             if t == PACK - 1:
-                ws_codes, ws_scales = quantize("ws", ws_grouped[:].rearrange("p t m j -> p (t m j)"), H)
+                ws_codes, ws_scales = quantize_slots("ws", ws_grouped)
             gate_times_value(gate_bank, value_bank, gated[1], "gate1_%d" % t, t, gate_slots[t])
-
-        wo_grouped = held("wo_grouped", [P, N, PACK], BF16, "bias_rows")
-        nc.scalar.copy(
-            out=wo_grouped[:].rearrange("p (c i) t -> p c t i", i=2),
-            in_=wo_raw[:].rearrange("p t (c i) -> p c t i", i=2),
-        )
 
         sensor_banks = {}
         for start in range(0, S, CHUNK):
@@ -253,20 +245,47 @@ def tile_list_traffic_gated_forecast_kernel(
                 )
             sensor_banks[start] = bank
 
-        def add_sensor_part(h_grouped, start, first):
+        h_grouped = [held("h_grouped%d" % first, [P, width, PACK], BF16) for first, width in OUT_GROUPS]
+
+        def chunk_operands(start):
             half, inside = divmod(start, HALF)
+            group = max(g for g, (first, width) in enumerate(OUT_GROUPS) if first <= start)
+            first = OUT_GROUPS[group][0]
+            return (
+                h_grouped[group][:, start - first : start - first + CHUNK, :],
+                gated[half][:, :, inside : inside + CHUNK],
+            )
+
+        for start in range(0, POOL_CHUNKS * CHUNK, CHUNK):
+            h_part, gated_part = chunk_operands(start)
+            parked = held("parked%d" % start, [P, CHUNK, PACK], F32)
+            nc.scalar.copy(out=parked[:], in_=sensor_banks[start][:].rearrange("p t j -> p j t"))
+            nc.gpsimd.tensor_tensor(h_part, gated_part.rearrange("p t j -> p j t"), parked[:], ALU.add)
+
+        def add_sensor_part(start):
+            h_part, gated_part = chunk_operands(start)
             nc.vector.tensor_tensor(
-                h_grouped[:, start - first : start - first + CHUNK, :].rearrange("p (c i) t -> p c t i", i=2),
+                h_part.rearrange("p (c i) t -> p c t i", i=2),
                 sensor_banks[start][:].rearrange("p t (c i) -> p c t i", i=2),
-                gated[half][:, :, inside : inside + CHUNK].rearrange("p t (c i) -> p c t i", i=2),
+                gated_part.rearrange("p t (c i) -> p c t i", i=2),
                 ALU.add,
             )
 
-        out_rows = out.rearrange("(c p) j -> p c j", p=P)
+        wo_grouped = held("wo_grouped", [P, N, PACK], BF16, "bias_rows")
+        nc.scalar.copy(
+            out=wo_grouped[:].rearrange("p (c i) t -> p c t i", i=2),
+            in_=wo_raw[:].rearrange("p t (c i) -> p c t i", i=2),
+        )
+        for start in range(POOL_CHUNKS * CHUNK, S - 2 * CHUNK, CHUNK):
+            add_sensor_part(start)
+        wo_codes, wo_scales = quantize(
+            "wo", wo_grouped[:].rearrange("p n t -> p (n t)"), N, "parked%d" % ((POOL_CHUNKS - 1) * CHUNK)
+        )
 
-        def forecast(h_grouped, first, width, last):
-            codes, scales = quantize("h%d" % first, h_grouped[:].rearrange("p j t -> p (j t)"), width)
-            result = held("result%d" % first, [P, N // P, width], F32)
+        def forecast(group):
+            first, width = OUT_GROUPS[group]
+            codes, scales = quantize("h%d" % first, h_grouped[group][:].rearrange("p j t -> p (j t)"), width)
+            banks = []
             for c in range(N // P):
                 cols = slice(c * P, (c + 1) * P)
                 bank = psum.tile([P, width], F32, name="bank")
@@ -274,25 +293,27 @@ def tile_list_traffic_gated_forecast_kernel(
                     out=bank[:], lhsT=wo_codes[:, cols].bitcast(FP8X4), lhsT_scale=wo_scales[:, cols],
                     rhs=codes[:].bitcast(FP8X4), rhs_scale=scales[:], start=True, stop=True,
                 )
-                if last and c == 1:
-                    nc.vector.tensor_scalar(
-                        result[:, c, :], bank[:], bias[:, PACK + c : PACK + c + 1], None, ALU.add
-                    )
+                banks.append(bank)
+            return banks
+
+        out_rows = out.rearrange("(c p) j -> p c j", p=P)
+
+        def store(group, banks, on_vector):
+            first, width = OUT_GROUPS[group]
+            result = held("result%d" % first, [P, N // P, width], F32)
+            for c in range(N // P):
+                column = bias[:, PACK + c : PACK + c + 1]
+                if on_vector[c]:
+                    nc.vector.tensor_scalar(result[:, c, :], banks[c][:], column, None, ALU.add)
                 else:
-                    nc.scalar.activation(
-                        result[:, c, :], bank[:], ACT.Identity, bias=bias[:, PACK + c : PACK + c + 1]
-                    )
+                    nc.scalar.activation(result[:, c, :], banks[c][:], ACT.Identity, bias=column)
             nc.sync.dma_start(out=out_rows[:, :, first : first + width], in_=result[:])
 
-        pending = None
-        for first, width in OUT_GROUPS:
-            h_grouped = held("h_grouped%d" % first, [P, width, PACK], BF16)
-            for start in range(first, first + width, CHUNK):
-                add_sensor_part(h_grouped, start, first)
-                if start == CHUNK:
-                    wo_codes, wo_scales = quantize("wo", wo_grouped[:].rearrange("p n t -> p (n t)"), N)
-                if pending is not None:
-                    forecast(*pending)
-                    pending = None
-            pending = (h_grouped, first, width, first + width == S)
-        forecast(*pending)
+        store(0, forecast(0), (False, False))
+        add_sensor_part(S - 2 * CHUNK)
+        late_banks = [forecast(1)]
+        add_sensor_part(S - CHUNK)
+        late_banks.append(forecast(2))
+        late_banks.append(forecast(3))
+        for group, banks in enumerate(late_banks, 1):
+            store(group, banks, (False, True))

@@ -23,7 +23,6 @@ K_PASS = P * PACK
 HALF = 512
 CHUNK = 128
 OUT_GROUPS = ((0, 512), (512, 256), (768, 128), (896, 128))
-POOL_CHUNKS = 1
 LIST_COLS = S // 16
 SENSOR_ROW = 8
 SECOND_ROW = 16
@@ -38,59 +37,64 @@ def tile_list_traffic_gated_forecast_kernel(
     nc = tc.nc
     with ExitStack() as ctx:
         keep = ctx.enter_context(tc.tile_pool(name="keep", bufs=1))
+        late = ctx.enter_context(tc.tile_pool(name="late", bufs=1))
         psum = ctx.enter_context(tc.psum_pool(name="psum", bufs=8))
 
         def held(name, shape, dtype, slot=""):
             return keep.tile(shape, dtype, name=name, tag=slot or name, align_bytes=64)
 
+        KIB = 1024
+        late_offset = {
+            "warm_out": 0, "road_first": 0, "wg_second": 16 * KIB, "wv_raw": 24 * KIB,
+            "bias_rows": 26 * KIB, "wv_scales_raw": 27 * KIB,
+            "ws_raw": 0, "v2_plane": 8 * KIB, "wo_raw": 16 * KIB,
+            "v_first": 28 * KIB, "road_scales": 30 * KIB, "road_second": 32 * KIB,
+        }
+
+        def late_tile(name, shape, dtype):
+            return late.tile(shape, dtype, name=name, align_bytes=64, offset=late_offset[name])
+
         road_list = keep.tile([P, LIST_COLS], U16, name="road_list")
         sensor_list = keep.tile([P, LIST_COLS], U16, name="sensor_list")
-        road_scales = held("road_scales", [P, T // 4], I32)
+        road_scales = late_tile("road_scales", [P, T // 4], I32)
         sensor_scales = held("sensor_scales", [P, T2 // 4], I32)
         wv_planes = held("wv_planes", [P, 2, H // 4], I32)
         second_plane = held("second_plane", [P, S // 4], I32)
-        bias_rows = held("bias_rows", [P, P], F32)
         identity = held("identity", [P, P], F32)
         bias = held("bias", [P, P - BIAS_ROW], F32)
         warm_in = held("warm_in", [P, 1], F32)
-        warm_out = held("warm_out", [P, 1], F32)
+        warm_out = late_tile("warm_out", [P, 28 * KIB // 4], F32)
 
         nc.vector.memset(road_scales[:], 0)
         nc.vector.memset(warm_in[:], 0.0)
-        nc.scalar.activation(warm_out[:], warm_in[:], ACT.Sigmoid)
-        nc.vector.memset(bias_rows[0:BIAS_ROW, :], 0.0)
         nc.vector.memset(wv_planes[:], 0)
         nc.vector.memset(second_plane[96:P, :], 0)
         nc.gpsimd.memset(sensor_scales[:], 0)
 
-        def load_words(name, words, columns, slot):
-            tile = held(name, [P, columns], I32, slot)
+        def load_words(tile, words):
             nc.sync.dma_start(out=tile[:], in_=words.rearrange("p t i -> p (t i)").bitcast(I32))
-            return tile
 
-        def load_weight(name, rows, slot=""):
-            tile = held(name, [P, PACK, H], F32, slot)
+        def load_weight(tile, rows):
             nc.sync.dma_start(out=tile[:], in_=rows.rearrange("(p j) c -> p j c", j=PACK))
-            return tile
 
         nc.sync.dma_start(road_list[:], offs)
         nc.sync.dma_start(sensor_list[:], offs2)
+        bias_rows = held("bias_rows", [P, P], F32)
+        nc.vector.memset(bias_rows[0:BIAS_ROW, :], 0.0)
         nc.sync.dma_start(
             out=bias_rows[BIAS_ROW : BIAS_ROW + PACK, :],
             in_=bg.rearrange("(b t q) -> t b q", t=PACK, q=8),
         )
         nc.sync.dma_start(out=bias_rows[BIAS_ROW + PACK : P, :], in_=bo.rearrange("(c p) -> c p", p=P))
-        wg_first = load_weight("wg_first", wg[0:K_PASS, :])
+
+        make_identity(nc, identity[:])
+        wg_first = held("wg_first", [P, PACK, H], F32)
+        load_weight(wg_first, wg[0:K_PASS, :])
+
         scale_rows = tab_scales.rearrange("a (quad r) t -> r quad a t", r=4)
         for r in range(4):
             nc.sync.dma_start(out=road_scales[r:P:SECOND_ROW, :], in_=scale_rows[r].bitcast(I32))
-        road_first = load_words("road_first", tab_words[0], T, "warm_in")
-        wv_scales_raw = held("wv_scales_raw", [P, 2, H // 4], I32, "warm_out")
-        for quad in range(4):
-            nc.sync.dma_start(
-                out=wv_scales_raw[32 * quad : 32 * quad + 4, :, :],
-                in_=wv_scales[:, 4 * quad : 4 * quad + 4, :].rearrange("a r n -> r a n").bitcast(I32),
-            )
+        nc.scalar.activation(warm_out[:, 0:1], warm_in[:], ACT.Sigmoid)
         for quad in range(4):
             first = 32 * quad + SENSOR_ROW
             nc.gpsimd.dma_start(
@@ -98,18 +102,25 @@ def tile_list_traffic_gated_forecast_kernel(
                 in_=tab2_scales[0, 4 * quad : 4 * quad + 4, :].bitcast(I32),
             )
 
-        make_identity(nc, identity[:])
+        road_first = late_tile("road_first", [P, T], I32)
+        load_words(road_first, tab_words[0])
+        wv_scales_raw = late_tile("wv_scales_raw", [P, 2, H // 4], I32)
+        for quad in range(4):
+            nc.sync.dma_start(
+                out=wv_scales_raw[32 * quad : 32 * quad + 4, :, :],
+                in_=wv_scales[:, 4 * quad : 4 * quad + 4, :].rearrange("a r n -> r a n").bitcast(I32),
+            )
+        wg_second = late_tile("wg_second", [P, PACK, H], F32)
+        load_weight(wg_second, wg[K_PASS:K, :])
+        wv_raw = late_tile("wv_raw", [P, 2, H // 2], I32)
+        nc.sync.dma_start(out=wv_raw[:], in_=wv_words.rearrange("a p n -> p a n").bitcast(I32))
         bias_bank = psum.tile([P, P], F32, name="bank")
         nc.tensor.transpose(bias_bank[:], bias_rows[:], identity[:])
         nc.scalar.copy(out=bias[:], in_=bias_bank[:, BIAS_ROW:P])
 
-        wg_second = load_weight("wg_second", wg[K_PASS:K, :], "bias_rows")
-        wv_raw = held("wv_raw", [P, 2, H // 2], I32, "identity")
-        nc.sync.dma_start(out=wv_raw[:], in_=wv_words.rearrange("a p n -> p a n").bitcast(I32))
-
         def gather(name, window, offsets, count, dtype, slot=""):
             words = count if dtype == U32 else count // 4
-            picked = held(name, [P, words], I32, slot)
+            picked = late_tile(name, [P, words], I32) if name in late_offset else held(name, [P, words], I32)
             nc.vector.tensor_copy(picked[:].bitcast(dtype), window[:].bitcast(dtype).indirect(offsets))
             return picked
 
@@ -131,30 +142,37 @@ def tile_list_traffic_gated_forecast_kernel(
         def quantize_slots(name, grouped):
             return quantize(name, grouped[:].rearrange("p t m j -> p (t m j)"), H)
 
-        wg_q = [quantize_slots("wg0", cast_permuted("wg0_grouped", wg_first))]
-        road_second = load_words("road_second", tab_words[1], T, "wg_first")
         packed_planes = gather("packed_planes", road_scales, road_list[:], S, U8)
         nc.scalar.dma_start(
             out=second_plane[0:PLANE_ROWS, :], in_=packed_planes[SECOND_ROW : SECOND_ROW + PLANE_ROWS, :]
         )
-        v_first = gather("v_first", road_first, road_list[:], S, U32, "road_scales")
+        road_second = late_tile("road_second", [P, T], I32)
+        load_words(road_second, tab_words[1])
+        v_first = gather("v_first", road_first, road_list[:], S, U32)
+        ws_raw = late_tile("ws_raw", [P, PACK, H], F32)
+        load_weight(ws_raw, ws)
+        v2_plane = gather("v2_plane", sensor_scales, sensor_list[:], S, U8)
         for quad in range(4):
             rows = slice(32 * quad, 32 * quad + 4)
             nc.vector.tensor_copy(
                 out=wv_planes[rows].rearrange("p a (t b w) -> p a t b w", t=PACK, w=2),
                 in_=wv_scales_raw[rows].rearrange("p a (b t w) -> p a t b w", t=PACK, w=2),
             )
-        v2_plane = gather("v2_plane", sensor_scales, sensor_list[:], S, U8, "warm_in")
-        wv_codes = held("wv_codes", [P, 2, H // 2], I32, "sensor_scales")
+        wg_q = [quantize_slots("wg0", cast_permuted("wg0_grouped", wg_first))]
+        sensor_words = held("sensor_words", [P, T2], I32, "wg_first")
+        load_words(sensor_words, tab2_words[0])
+        wv_codes = held("wv_codes", [P, 2, H // 2], I32)
         for a in range(2):
             nc.vector.tensor_copy(
                 out=wv_codes[:, a, :].rearrange("p (t b w) -> p t b w", t=PACK, w=4),
                 in_=wv_raw[:, a, :].rearrange("p (b t w) -> p t b w", t=PACK, w=4),
             )
-
         wg_q.append(quantize_slots("wg1", cast_permuted("wg1_grouped", wg_second)))
-        ws_raw = load_weight("ws_raw", ws, "bias_rows")
-        sensor_words = load_words("sensor_words", tab2_words[0], T2, "identity")
+
+        wo_raw = late_tile("wo_raw", [P, PACK, N], F32)
+        wo_rows = wo.rearrange("(b t q) n -> t b q n", t=PACK, q=8)
+        for t in range(PACK):
+            nc.sync.dma_start(out=wo_raw[:, t, :], in_=wo_rows[t])
 
         v_second = []
 
@@ -197,13 +215,7 @@ def tile_list_traffic_gated_forecast_kernel(
         half_cols = LIST_COLS // 2
         for half in range(2):
             offsets = road_list[:, half * half_cols : (half + 1) * half_cols]
-            slot = "wg1_grouped" if half == 0 else ""
-            v_second.append(gather("v_second%d" % half, road_second, offsets, HALF, U32, slot))
-
-        wo_raw = held("wo_raw", [P, PACK, N], F32, "wg_first")
-        wo_rows = wo.rearrange("(b t q) n -> t b q n", t=PACK, q=8)
-        for t in range(PACK):
-            nc.sync.dma_start(out=wo_raw[:, t, :], in_=wo_rows[t])
+            v_second.append(gather("v_second%d" % half, road_second, offsets, HALF, U32))
 
         gated = [held("gated0", [P, PACK, HALF], F32)]
         for t in range(PACK):
@@ -211,14 +223,7 @@ def tile_list_traffic_gated_forecast_kernel(
             value_pass(value_banks[t], 1, 0, t)
             gate_times_value(gate_banks[t], value_banks[t], gated[0], "gate0_%d" % t, t)
 
-        v2 = []
-        for half in range(2):
-            offsets = sensor_list[:, half * half_cols : (half + 1) * half_cols]
-            v2.append(gather("v2_%d" % half, sensor_words, offsets, HALF, U32, "gate0_%d" % (2 + half)))
-
-        gated.append(held("gated1", [P, PACK, HALF], F32, "identity"))
-        ws_grouped = cast_permuted("ws_grouped", ws_raw, "gate0_1")
-        gate_slots = ("", "", "bias_rows", "gate0_1")
+        gated.append(held("gated1", [P, PACK, HALF], F32))
         for t in range(PACK):
             gate_bank = psum.tile([P, HALF], F32, name="bank")
             value_bank = psum.tile([P, HALF], F32, name="bank")
@@ -226,9 +231,13 @@ def tile_list_traffic_gated_forecast_kernel(
                 gate_pass(gate_bank, a, 1, t)
             for a in range(2):
                 value_pass(value_bank, a, 1, t)
-            if t == PACK - 1:
-                ws_codes, ws_scales = quantize_slots("ws", ws_grouped)
-            gate_times_value(gate_bank, value_bank, gated[1], "gate1_%d" % t, t, gate_slots[t])
+            gate_times_value(gate_bank, value_bank, gated[1], "gate1_%d" % t, t)
+
+        ws_codes, ws_scales = quantize_slots("ws", cast_permuted("ws_grouped", ws_raw))
+        v2 = []
+        for half in range(2):
+            offsets = sensor_list[:, half * half_cols : (half + 1) * half_cols]
+            v2.append(gather("v2_%d" % half, sensor_words, offsets, HALF, U32))
 
         sensor_banks = {}
         for start in range(0, S, CHUNK):
@@ -245,47 +254,28 @@ def tile_list_traffic_gated_forecast_kernel(
                 )
             sensor_banks[start] = bank
 
-        h_grouped = [held("h_grouped%d" % first, [P, width, PACK], BF16) for first, width in OUT_GROUPS]
-
-        def chunk_operands(start):
-            half, inside = divmod(start, HALF)
-            group = max(g for g, (first, width) in enumerate(OUT_GROUPS) if first <= start)
-            first = OUT_GROUPS[group][0]
-            return (
-                h_grouped[group][:, start - first : start - first + CHUNK, :],
-                gated[half][:, :, inside : inside + CHUNK],
-            )
-
-        for start in range(0, POOL_CHUNKS * CHUNK, CHUNK):
-            h_part, gated_part = chunk_operands(start)
-            parked = held("parked%d" % start, [P, CHUNK, PACK], F32)
-            nc.scalar.copy(out=parked[:], in_=sensor_banks[start][:].rearrange("p t j -> p j t"))
-            nc.gpsimd.tensor_tensor(h_part, gated_part.rearrange("p t j -> p j t"), parked[:], ALU.add)
-
-        def add_sensor_part(start):
-            h_part, gated_part = chunk_operands(start)
-            nc.vector.tensor_tensor(
-                h_part.rearrange("p (c i) t -> p c t i", i=2),
-                sensor_banks[start][:].rearrange("p t (c i) -> p c t i", i=2),
-                gated_part.rearrange("p t (c i) -> p c t i", i=2),
-                ALU.add,
-            )
-
-        wo_grouped = held("wo_grouped", [P, N, PACK], BF16, "bias_rows")
+        wo_grouped = held("wo_grouped", [P, N, PACK], BF16)
         nc.scalar.copy(
             out=wo_grouped[:].rearrange("p (c i) t -> p c t i", i=2),
             in_=wo_raw[:].rearrange("p t (c i) -> p c t i", i=2),
         )
-        for start in range(POOL_CHUNKS * CHUNK, S - 2 * CHUNK, CHUNK):
-            add_sensor_part(start)
-        wo_codes, wo_scales = quantize(
-            "wo", wo_grouped[:].rearrange("p n t -> p (n t)"), N, "parked%d" % ((POOL_CHUNKS - 1) * CHUNK)
-        )
+        wo_codes, wo_scales = quantize("wo", wo_grouped[:].rearrange("p n t -> p (n t)"), N)
 
-        def forecast(group):
-            first, width = OUT_GROUPS[group]
-            codes, scales = quantize("h%d" % first, h_grouped[group][:].rearrange("p j t -> p (j t)"), width)
-            banks = []
+        out_rows = out.rearrange("(c p) j -> p c j", p=P)
+        for first, width in OUT_GROUPS:
+            h_grouped = held("h_grouped%d" % first, [P, width, PACK], BF16)
+            for start in range(first, first + width, CHUNK):
+                half, inside = divmod(start, HALF)
+                bank = sensor_banks[start]
+                h_part = h_grouped[:, start - first : start - first + CHUNK, :]
+                nc.vector.tensor_tensor(
+                    h_part.rearrange("p (c i) t -> p c t i", i=2),
+                    bank[:].rearrange("p t (c i) -> p c t i", i=2),
+                    gated[half][:, :, inside : inside + CHUNK].rearrange("p t (c i) -> p c t i", i=2),
+                    ALU.add,
+                )
+            codes, scales = quantize("h%d" % first, h_grouped[:].rearrange("p j t -> p (j t)"), width)
+            result = held("result%d" % first, [P, N // P, width], F32)
             for c in range(N // P):
                 cols = slice(c * P, (c + 1) * P)
                 bank = psum.tile([P, width], F32, name="bank")
@@ -293,27 +283,9 @@ def tile_list_traffic_gated_forecast_kernel(
                     out=bank[:], lhsT=wo_codes[:, cols].bitcast(FP8X4), lhsT_scale=wo_scales[:, cols],
                     rhs=codes[:].bitcast(FP8X4), rhs_scale=scales[:], start=True, stop=True,
                 )
-                banks.append(bank)
-            return banks
-
-        out_rows = out.rearrange("(c p) j -> p c j", p=P)
-
-        def store(group, banks, on_vector):
-            first, width = OUT_GROUPS[group]
-            result = held("result%d" % first, [P, N // P, width], F32)
-            for c in range(N // P):
                 column = bias[:, PACK + c : PACK + c + 1]
-                if on_vector[c]:
-                    nc.vector.tensor_scalar(result[:, c, :], banks[c][:], column, None, ALU.add)
+                if first + width == S and c == 1:
+                    nc.vector.tensor_scalar(result[:, c, :], bank[:], column, None, ALU.add)
                 else:
-                    nc.scalar.activation(result[:, c, :], banks[c][:], ACT.Identity, bias=column)
+                    nc.scalar.activation(result[:, c, :], bank[:], ACT.Identity, bias=column)
             nc.sync.dma_start(out=out_rows[:, :, first : first + width], in_=result[:])
-
-        store(0, forecast(0), (False, False))
-        add_sensor_part(S - 2 * CHUNK)
-        late_banks = [forecast(1)]
-        add_sensor_part(S - CHUNK)
-        late_banks.append(forecast(2))
-        late_banks.append(forecast(3))
-        for group, banks in enumerate(late_banks, 1):
-            store(group, banks, (False, True))

@@ -45,10 +45,9 @@ def tile_list_traffic_gated_forecast_kernel(
 
         KIB = 1024
         late_offset = {
-            "warm_out": 0, "road_first": 0, "wg_second": 16 * KIB, "wv_raw": 24 * KIB,
-            "bias_rows": 26 * KIB, "wv_scales_raw": 27 * KIB,
-            "ws_raw": 0, "v2_plane": 8 * KIB, "wo_raw": 16 * KIB,
-            "v_first": 28 * KIB, "road_scales": 30 * KIB, "road_second": 32 * KIB,
+            "warm_out": 0, "road_first": 0, "ws_raw": 0, "sensor_words": 8 * KIB,
+            "v2_plane": 16 * KIB, "wv_scales_raw": 18 * KIB, "road_second": 18 * KIB, "wo_raw": 18 * KIB,
+            "road_scales": 34 * KIB, "wg_second": 34 * KIB,
         }
 
         def late_tile(name, shape, dtype):
@@ -61,18 +60,17 @@ def tile_list_traffic_gated_forecast_kernel(
         wv_planes = held("wv_planes", [P, 2, H // 4], I32)
         second_plane = held("second_plane", [P, S // 4], I32)
         identity = held("identity", [P, P], F32)
-        bias = held("bias", [P, P - BIAS_ROW], F32)
         warm_in = held("warm_in", [P, 1], F32)
-        warm_out = late_tile("warm_out", [P, 28 * KIB // 4], F32)
+        warm_out = late_tile("warm_out", [P, 1], F32)
 
-        nc.vector.memset(road_scales[:], 0)
+        nc.gpsimd.memset(road_scales[:, T // 8 : T // 4], 0)
+        nc.vector.memset(road_scales[:, 0 : T // 8], 0)
         nc.vector.memset(warm_in[:], 0.0)
         nc.vector.memset(wv_planes[:], 0)
         nc.vector.memset(second_plane[96:P, :], 0)
-        nc.gpsimd.memset(sensor_scales[:], 0)
 
         def load_words(tile, words):
-            nc.sync.dma_start(out=tile[:], in_=words.rearrange("p t i -> p (t i)").bitcast(I32))
+            nc.sync.dma_start(out=tile, in_=words.rearrange("p t i -> p (t i)").bitcast(I32))
 
         def load_weight(tile, rows):
             nc.sync.dma_start(out=tile[:], in_=rows.rearrange("(p j) c -> p j c", j=PACK))
@@ -81,47 +79,51 @@ def tile_list_traffic_gated_forecast_kernel(
         nc.sync.dma_start(sensor_list[:], offs2)
         bias_rows = held("bias_rows", [P, P], F32)
         nc.vector.memset(bias_rows[0:BIAS_ROW, :], 0.0)
-        nc.sync.dma_start(
+        nc.gpsimd.dma_start(
             out=bias_rows[BIAS_ROW : BIAS_ROW + PACK, :],
             in_=bg.rearrange("(b t q) -> t b q", t=PACK, q=8),
         )
-        nc.sync.dma_start(out=bias_rows[BIAS_ROW + PACK : P, :], in_=bo.rearrange("(c p) -> c p", p=P))
+        nc.gpsimd.dma_start(out=bias_rows[BIAS_ROW + PACK : P, :], in_=bo.rearrange("(c p) -> c p", p=P))
 
         make_identity(nc, identity[:])
-        wg_first = held("wg_first", [P, PACK, H], F32)
-        load_weight(wg_first, wg[0:K_PASS, :])
-
-        scale_rows = tab_scales.rearrange("a (quad r) t -> r quad a t", r=4)
-        for r in range(4):
-            nc.sync.dma_start(out=road_scales[r:P:SECOND_ROW, :], in_=scale_rows[r].bitcast(I32))
-        nc.scalar.activation(warm_out[:, 0:1], warm_in[:], ACT.Sigmoid)
-        for quad in range(4):
-            first = 32 * quad + SENSOR_ROW
-            nc.gpsimd.dma_start(
-                out=sensor_scales[first : first + 4, :],
-                in_=tab2_scales[0, 4 * quad : 4 * quad + 4, :].bitcast(I32),
-            )
-
-        road_first = late_tile("road_first", [P, T], I32)
-        load_words(road_first, tab_words[0])
         wv_scales_raw = late_tile("wv_scales_raw", [P, 2, H // 4], I32)
         for quad in range(4):
             nc.sync.dma_start(
                 out=wv_scales_raw[32 * quad : 32 * quad + 4, :, :],
                 in_=wv_scales[:, 4 * quad : 4 * quad + 4, :].rearrange("a r n -> r a n").bitcast(I32),
             )
-        wg_second = late_tile("wg_second", [P, PACK, H], F32)
-        load_weight(wg_second, wg[K_PASS:K, :])
-        wv_raw = late_tile("wv_raw", [P, 2, H // 2], I32)
+        wg_first = held("wg_first", [P, PACK, H], F32)
+        load_weight(wg_first, wg[0:K_PASS, :])
+        wv_raw = held("wv_raw", [P, 2, H // 2], I32)
         nc.sync.dma_start(out=wv_raw[:], in_=wv_words.rearrange("a p n -> p a n").bitcast(I32))
-        bias_bank = psum.tile([P, P], F32, name="bank")
-        nc.tensor.transpose(bias_bank[:], bias_rows[:], identity[:])
-        nc.scalar.copy(out=bias[:], in_=bias_bank[:, BIAS_ROW:P])
+
+        scale_rows = tab_scales.rearrange("a (quad r) t -> r quad a t", r=4)
+        for r in range(4):
+            nc.sync.dma_start(out=road_scales[r:P:SECOND_ROW, :], in_=scale_rows[r].bitcast(I32))
+        nc.scalar.activation(warm_out[:, 0:1], warm_in[:], ACT.Sigmoid)
+        road_first = late_tile("road_first", [P, T + S // 4], I32)
+        load_words(road_first[:, 0:T], tab_words[0])
+        nc.vector.memset(sensor_scales[:], 0)
+        for quad in range(4):
+            first = 32 * quad + SENSOR_ROW
+            nc.sync.dma_start(
+                out=sensor_scales[first : first + 4, :],
+                in_=tab2_scales[0, 4 * quad : 4 * quad + 4, :].bitcast(I32),
+            )
+
+        for quad in range(4):
+            rows = slice(32 * quad, 32 * quad + 4)
+            nc.vector.tensor_copy(
+                out=wv_planes[rows].rearrange("p a (t b w) -> p a t b w", t=PACK, w=2),
+                in_=wv_scales_raw[rows].rearrange("p a (b t w) -> p a t b w", t=PACK, w=2),
+            )
+        road_second = late_tile("road_second", [P, T], I32)
+        load_words(road_second[:], tab_words[1])
 
         def gather(name, window, offsets, count, dtype, slot=""):
             words = count if dtype == U32 else count // 4
             picked = late_tile(name, [P, words], I32) if name in late_offset else held(name, [P, words], I32)
-            nc.vector.tensor_copy(picked[:].bitcast(dtype), window[:].bitcast(dtype).indirect(offsets))
+            nc.vector.tensor_copy(picked[:].bitcast(dtype), window.bitcast(dtype).indirect(offsets))
             return picked
 
         def quantize(name, grouped, width, slot=""):
@@ -130,51 +132,57 @@ def tile_list_traffic_gated_forecast_kernel(
             nc.vector.quantize_mx(out=codes[:].bitcast(FP8X4), scales=scales[:], in_=grouped)
             return codes, scales
 
-        def cast_permuted(name, raw, slot=""):
-            grouped = held(name, [P, PACK, P, PACK], BF16, slot)
+        def cast_slot(engine, grouped, raw, t):
             source = raw[:].rearrange("p j (b t u i) -> p t b u j i", t=PACK, u=4, i=2)
-            for t in range(PACK):
-                nc.scalar.copy(
-                    out=grouped[:, t].rearrange("p (b u i) j -> p b u j i", u=4, i=2), in_=source[:, t]
-                )
-            return grouped
+            target = grouped.rearrange("p (b u i) j -> p b u j i", u=4, i=2)
+            if engine == "scalar":
+                nc.scalar.copy(out=target, in_=source[:, t])
+            else:
+                nc.vector.tensor_copy(out=target, in_=source[:, t])
 
         def quantize_slots(name, grouped):
             return quantize(name, grouped[:].rearrange("p t m j -> p (t m j)"), H)
 
-        packed_planes = gather("packed_planes", road_scales, road_list[:], S, U8)
-        nc.scalar.dma_start(
+        packed_planes = gather("packed_planes", road_scales[:], road_list[:], S, U8)
+        nc.sync.dma_start(
             out=second_plane[0:PLANE_ROWS, :], in_=packed_planes[SECOND_ROW : SECOND_ROW + PLANE_ROWS, :]
         )
-        road_second = late_tile("road_second", [P, T], I32)
-        load_words(road_second, tab_words[1])
-        v_first = gather("v_first", road_first, road_list[:], S, U32)
-        ws_raw = late_tile("ws_raw", [P, PACK, H], F32)
-        load_weight(ws_raw, ws)
-        v2_plane = gather("v2_plane", sensor_scales, sensor_list[:], S, U8)
-        for quad in range(4):
-            rows = slice(32 * quad, 32 * quad + 4)
-            nc.vector.tensor_copy(
-                out=wv_planes[rows].rearrange("p a (t b w) -> p a t b w", t=PACK, w=2),
-                in_=wv_scales_raw[rows].rearrange("p a (b t w) -> p a t b w", t=PACK, w=2),
-            )
-        wg_q = [quantize_slots("wg0", cast_permuted("wg0_grouped", wg_first))]
-        sensor_words = held("sensor_words", [P, T2], I32, "wg_first")
-        load_words(sensor_words, tab2_words[0])
+        wg_second = late_tile("wg_second", [P, PACK, H], F32)
+        load_weight(wg_second, wg[K_PASS:K, :])
+        wg_q = {}
+        wg0_grouped = held("wg0_grouped", [P, PACK, P, PACK], BF16)
+        for t in range(PACK):
+            cast_slot("scalar", wg0_grouped[:, t], wg_first, t)
+        codes, scales = quantize_slots("wg0", wg0_grouped)
+        for t in range(PACK):
+            wg_q[0, t] = (codes[:, t * P : (t + 1) * P], scales[:, t * P : (t + 1) * P])
+        bias = held("bias", [P, P - BIAS_ROW], F32, "wg_first")
+        bias_bank = psum.tile([P, P], F32, name="bank")
+        nc.tensor.transpose(bias_bank[:], bias_rows[:], identity[:])
+        nc.scalar.copy(out=bias[:], in_=bias_bank[:, BIAS_ROW:P])
+
         wv_codes = held("wv_codes", [P, 2, H // 2], I32)
         for a in range(2):
             nc.vector.tensor_copy(
                 out=wv_codes[:, a, :].rearrange("p (t b w) -> p t b w", t=PACK, w=4),
                 in_=wv_raw[:, a, :].rearrange("p (b t w) -> p t b w", t=PACK, w=4),
             )
-        wg_q.append(quantize_slots("wg1", cast_permuted("wg1_grouped", wg_second)))
+        v_first = gather("v_first", road_first[:, 0:T], road_list[:], S, U32)
+        ws_raw = late_tile("ws_raw", [P, PACK, H], F32)
+        load_weight(ws_raw, ws)
+        sensor_words = late_tile("sensor_words", [P, T2], I32)
+        load_words(sensor_words[:], tab2_words[0])
+        v2_plane = gather("v2_plane", sensor_scales[:], sensor_list[:], S, U8)
 
+        half_cols = LIST_COLS // 2
+        v_second = {}
+        for half in (1, 0):
+            offsets = road_list[:, half * half_cols : (half + 1) * half_cols]
+            v_second[half] = gather("v_second%d" % half, road_second[:], offsets, HALF, U32)
         wo_raw = late_tile("wo_raw", [P, PACK, N], F32)
         wo_rows = wo.rearrange("(b t q) n -> t b q n", t=PACK, q=8)
         for t in range(PACK):
             nc.sync.dma_start(out=wo_raw[:, t, :], in_=wo_rows[t])
-
-        v_second = []
 
         def road_operand(a, half):
             cols = slice(half * HALF, (half + 1) * HALF)
@@ -183,11 +191,10 @@ def tile_list_traffic_gated_forecast_kernel(
             return v_second[half][:].bitcast(FP8X4), second_plane[:].bitcast(U8)[:, cols]
 
         def gate_pass(bank, a, half, t):
-            codes, scales = wg_q[a]
-            cols = slice(t * P, (t + 1) * P)
+            codes, scales = wg_q[a, t]
             rhs, rhs_scale = road_operand(a, half)
             nc.tensor.matmul_mx(
-                out=bank[:], lhsT=codes[:, cols].bitcast(FP8X4), lhsT_scale=scales[:, cols],
+                out=bank[:], lhsT=codes.bitcast(FP8X4), lhsT_scale=scales,
                 rhs=rhs, rhs_scale=rhs_scale, start=(a == 0), stop=(a == 1),
             )
 
@@ -200,44 +207,59 @@ def tile_list_traffic_gated_forecast_kernel(
                 rhs=rhs, rhs_scale=rhs_scale, start=(a == 0), stop=(a == 1),
             )
 
-        def gate_times_value(gate_bank, value_bank, gated, name, t, slot=""):
-            gate = held(name, [P, HALF], F32, slot)
-            nc.scalar.activation(gate[:], gate_bank[:], ACT.Sigmoid, bias=bias[:, t : t + 1])
-            nc.vector.tensor_tensor(gated[:, t, :], value_bank[:], gate[:], ALU.mult)
-
-        gate_banks = [psum.tile([P, HALF], F32, name="bank") for t in range(PACK)]
-        value_banks = [psum.tile([P, HALF], F32, name="bank") for t in range(PACK)]
+        value_banks = {}
+        for half in (1, 0):
+            for t in range(PACK):
+                value_banks[half, t] = psum.tile([P, HALF], F32, name="bank")
+                value_pass(value_banks[half, t], 0, half, t)
+        parked = []
         for t in range(PACK):
-            gate_pass(gate_banks[t], 0, 0, t)
+            value_pass(value_banks[1, t], 1, 1, t)
+            parked.append(held("parked%d" % t, [P, HALF], F32))
+            nc.scalar.copy(out=parked[t][:], in_=value_banks[1, t][:])
         for t in range(PACK):
-            value_pass(value_banks[t], 0, 0, t)
+            value_pass(value_banks[0, t], 1, 0, t)
 
-        half_cols = LIST_COLS // 2
-        for half in range(2):
-            offsets = road_list[:, half * half_cols : (half + 1) * half_cols]
-            v_second.append(gather("v_second%d" % half, road_second, offsets, HALF, U32))
-
-        gated = [held("gated0", [P, PACK, HALF], F32)]
+        gate_banks = {}
         for t in range(PACK):
-            gate_pass(gate_banks[t], 1, 0, t)
-            value_pass(value_banks[t], 1, 0, t)
-            gate_times_value(gate_banks[t], value_banks[t], gated[0], "gate0_%d" % t, t)
-
-        gated.append(held("gated1", [P, PACK, HALF], F32))
+            gate_banks[0, t] = psum.tile([P, HALF], F32, name="bank")
+            gate_pass(gate_banks[0, t], 0, 0, t)
+        wg1_grouped = [held("wg1_grouped%d" % t, [P, P, PACK], BF16) for t in range(PACK)]
         for t in range(PACK):
-            gate_bank = psum.tile([P, HALF], F32, name="bank")
-            value_bank = psum.tile([P, HALF], F32, name="bank")
+            cast_slot("vector", wg1_grouped[t][:], wg_second, t)
+        for t in range(PACK):
+            codes, scales = quantize("wg1_%d" % t, wg1_grouped[t][:].rearrange("p m j -> p (m j)"), P)
+            wg_q[1, t] = (codes[:], scales[:])
+
+        gated = [held("gated%d" % half, [P, PACK, HALF], F32) for half in range(2)]
+
+        def sigmoid_gate(half, t):
+            gate = held("gate%d_%d" % (half, t), [P, HALF], F32)
+            nc.scalar.activation(gate[:], gate_banks[half, t][:], ACT.Sigmoid, bias=bias[:, t : t + 1])
+            return gate
+
+        for t in range(PACK):
+            gate_pass(gate_banks[0, t], 1, 0, t)
+            nc.vector.tensor_tensor(gated[0][:, t, :], value_banks[0, t][:], sigmoid_gate(0, t)[:], ALU.mult)
+
+        ws_grouped = held("ws_grouped", [P, PACK, P, PACK], BF16)
+        ws_source = ws_raw[:].rearrange("p j (b t q) -> p t b q j", t=PACK, q=8)
+        for t in range(PACK):
+            nc.gpsimd.tensor_scalar(
+                ws_grouped[:, t].rearrange("p (b q) j -> p b q j", q=8), ws_source[:, t], 1.0, 0.0, ALU.mult, ALU.add
+            )
+        for t in range(PACK):
+            gate_banks[1, t] = psum.tile([P, HALF], F32, name="bank")
             for a in range(2):
-                gate_pass(gate_bank, a, 1, t)
-            for a in range(2):
-                value_pass(value_bank, a, 1, t)
-            gate_times_value(gate_bank, value_bank, gated[1], "gate1_%d" % t, t)
+                gate_pass(gate_banks[1, t], a, 1, t)
+            nc.gpsimd.tensor_tensor(gated[1][:, t, :], parked[t][:], sigmoid_gate(1, t)[:], ALU.mult)
 
-        ws_codes, ws_scales = quantize_slots("ws", cast_permuted("ws_grouped", ws_raw))
         v2 = []
         for half in range(2):
             offsets = sensor_list[:, half * half_cols : (half + 1) * half_cols]
-            v2.append(gather("v2_%d" % half, sensor_words, offsets, HALF, U32))
+            v2.append(gather("v2_%d" % half, sensor_words[:], offsets, HALF, U32))
+            if half == 0:
+                ws_codes, ws_scales = quantize_slots("ws", ws_grouped)
 
         sensor_banks = {}
         for start in range(0, S, CHUNK):

@@ -38,7 +38,10 @@ def tile_list_traffic_gated_forecast_kernel(
     with ExitStack() as ctx:
         keep = ctx.enter_context(tc.tile_pool(name="keep", bufs=1))
         late = ctx.enter_context(tc.tile_pool(name="late", bufs=1))
-        psum = ctx.enter_context(tc.psum_pool(name="psum", bufs=8))
+        psum = ctx.enter_context(tc.psum_pool(name="psum", bufs=1))
+
+        def bank_tile(index, shape):
+            return psum.tile(shape, F32, name="bank%d" % index)
 
         def held(name, shape, dtype, slot=""):
             return keep.tile(shape, dtype, name=name, tag=slot or name, align_bytes=64)
@@ -157,7 +160,7 @@ def tile_list_traffic_gated_forecast_kernel(
         for t in range(PACK):
             wg_q[0, t] = (codes[:, t * P : (t + 1) * P], scales[:, t * P : (t + 1) * P])
         bias = held("bias", [P, P - BIAS_ROW], F32, "wg_first")
-        bias_bank = psum.tile([P, P], F32, name="bank")
+        bias_bank = bank_tile(7, [P, P])
         nc.tensor.transpose(bias_bank[:], bias_rows[:], identity[:])
         nc.scalar.copy(out=bias[:], in_=bias_bank[:, BIAS_ROW:P])
 
@@ -176,7 +179,7 @@ def tile_list_traffic_gated_forecast_kernel(
 
         half_cols = LIST_COLS // 2
         v_second = {}
-        for half in (1, 0):
+        for half in range(2):
             offsets = road_list[:, half * half_cols : (half + 1) * half_cols]
             v_second[half] = gather("v_second%d" % half, road_second[:], offsets, HALF, U32)
         wo_raw = late_tile("wo_raw", [P, PACK, N], F32)
@@ -190,12 +193,12 @@ def tile_list_traffic_gated_forecast_kernel(
                 return v_first[:, cols].bitcast(FP8X4), packed_planes[:].bitcast(U8)[:, cols]
             return v_second[half][:].bitcast(FP8X4), second_plane[:].bitcast(U8)[:, cols]
 
-        def gate_pass(bank, a, half, t):
+        def gate_pass(bank, a, half, t, opens):
             codes, scales = wg_q[a, t]
             rhs, rhs_scale = road_operand(a, half)
             nc.tensor.matmul_mx(
                 out=bank[:], lhsT=codes.bitcast(FP8X4), lhsT_scale=scales,
-                rhs=rhs, rhs_scale=rhs_scale, start=(a == 0), stop=(a == 1),
+                rhs=rhs, rhs_scale=rhs_scale, start=opens, stop=not opens,
             )
 
         def value_pass(bank, a, half, t):
@@ -208,26 +211,21 @@ def tile_list_traffic_gated_forecast_kernel(
             )
 
         value_banks = {}
-        for half in (1, 0):
-            for t in range(PACK):
-                value_banks[half, t] = psum.tile([P, HALF], F32, name="bank")
-                value_pass(value_banks[half, t], 0, half, t)
-        parked = []
+        gate_banks = {}
         for t in range(PACK):
-            value_pass(value_banks[1, t], 1, 1, t)
-            parked.append(held("parked%d" % t, [P, HALF], F32))
-            nc.scalar.copy(out=parked[t][:], in_=value_banks[1, t][:])
+            gate_banks[0, t] = bank_tile(t, [P, HALF])
+            gate_pass(gate_banks[0, t], 0, 0, t, True)
+        for t in range(PACK):
+            value_banks[0, t] = bank_tile(PACK + t, [P, HALF])
+            value_pass(value_banks[0, t], 0, 0, t)
         for t in range(PACK):
             value_pass(value_banks[0, t], 1, 0, t)
 
-        gate_banks = {}
-        for t in range(PACK):
-            gate_banks[0, t] = psum.tile([P, HALF], F32, name="bank")
-            gate_pass(gate_banks[0, t], 0, 0, t)
         wg1_grouped = [held("wg1_grouped%d" % t, [P, P, PACK], BF16) for t in range(PACK)]
+        cast_slot("scalar", wg1_grouped[0][:], wg_second, 0)
         for t in range(PACK):
-            cast_slot("vector", wg1_grouped[t][:], wg_second, t)
-        for t in range(PACK):
+            if t + 1 < PACK:
+                cast_slot("scalar" if t == 0 else "vector", wg1_grouped[t + 1][:], wg_second, t + 1)
             codes, scales = quantize("wg1_%d" % t, wg1_grouped[t][:].rearrange("p m j -> p (m j)"), P)
             wg_q[1, t] = (codes[:], scales[:])
 
@@ -239,7 +237,7 @@ def tile_list_traffic_gated_forecast_kernel(
             return gate
 
         for t in range(PACK):
-            gate_pass(gate_banks[0, t], 1, 0, t)
+            gate_pass(gate_banks[0, t], 1, 0, t, False)
             nc.vector.tensor_tensor(gated[0][:, t, :], value_banks[0, t][:], sigmoid_gate(0, t)[:], ALU.mult)
 
         ws_grouped = held("ws_grouped", [P, PACK, P, PACK], BF16)
@@ -249,10 +247,15 @@ def tile_list_traffic_gated_forecast_kernel(
                 ws_grouped[:, t].rearrange("p (b q) j -> p b q j", q=8), ws_source[:, t], 1.0, 0.0, ALU.mult, ALU.add
             )
         for t in range(PACK):
-            gate_banks[1, t] = psum.tile([P, HALF], F32, name="bank")
+            value_banks[1, t] = bank_tile((0, 4, 5, 0)[t], [P, HALF])
             for a in range(2):
-                gate_pass(gate_banks[1, t], a, 1, t)
-            nc.gpsimd.tensor_tensor(gated[1][:, t, :], parked[t][:], sigmoid_gate(1, t)[:], ALU.mult)
+                value_pass(value_banks[1, t], a, 1, t)
+            gate_banks[1, t] = bank_tile((1, 2, 3, 1)[t], [P, HALF])
+            for a in range(2):
+                gate_pass(gate_banks[1, t], a, 1, t, a == 0)
+            parked = held("parked%d" % t, [P, HALF], F32)
+            nc.scalar.copy(out=parked[:], in_=value_banks[1, t][:])
+            nc.gpsimd.tensor_tensor(gated[1][:, t, :], parked[:], sigmoid_gate(1, t)[:], ALU.mult)
 
         v2 = []
         for half in range(2):
@@ -264,7 +267,7 @@ def tile_list_traffic_gated_forecast_kernel(
         sensor_banks = {}
         for start in range(0, S, CHUNK):
             half, inside = divmod(start, HALF)
-            bank = psum.tile([P, PACK, CHUNK], F32, name="bank")
+            bank = bank_tile((6, 7, 4, 2, 5, 3, 0, 1)[start // CHUNK], [P, PACK, CHUNK])
             for t in range(PACK):
                 cols = slice(t * P, (t + 1) * P)
                 nc.tensor.matmul_mx(
@@ -284,7 +287,7 @@ def tile_list_traffic_gated_forecast_kernel(
         wo_codes, wo_scales = quantize("wo", wo_grouped[:].rearrange("p n t -> p (n t)"), N)
 
         out_rows = out.rearrange("(c p) j -> p c j", p=P)
-        for first, width in OUT_GROUPS:
+        for group, (first, width) in enumerate(OUT_GROUPS):
             h_grouped = held("h_grouped%d" % first, [P, width, PACK], BF16)
             for start in range(first, first + width, CHUNK):
                 half, inside = divmod(start, HALF)
@@ -300,7 +303,7 @@ def tile_list_traffic_gated_forecast_kernel(
             result = held("result%d" % first, [P, N // P, width], F32)
             for c in range(N // P):
                 cols = slice(c * P, (c + 1) * P)
-                bank = psum.tile([P, width], F32, name="bank")
+                bank = bank_tile((6, 7, 4, 2, 5, 3, 0, 1)[2 * group + c], [P, width])
                 nc.tensor.matmul_mx(
                     out=bank[:], lhsT=wo_codes[:, cols].bitcast(FP8X4), lhsT_scale=wo_scales[:, cols],
                     rhs=codes[:].bitcast(FP8X4), rhs_scale=scales[:], start=True, stop=True,

@@ -22,11 +22,10 @@ PACK = 4
 K_PASS = P * PACK
 HALF = 512
 CHUNK = 128
-OUT_GROUPS = ((0, 512), (512, 256), (768, 128), (896, 128))
+OUT_GROUPS = ((0, 256), (256, 256), (512, 128), (640, 128), (768, 128), (896, 128))
+POOL_CHUNK = 896
 LIST_COLS = S // 16
 SENSOR_ROW = 8
-SECOND_ROW = 16
-PLANE_ROWS = 100
 BIAS_ROW = 122
 
 
@@ -48,9 +47,9 @@ def tile_list_traffic_gated_forecast_kernel(
 
         KIB = 1024
         late_offset = {
-            "warm_out": 0, "road_first": 0, "ws_raw": 0, "sensor_words": 8 * KIB,
-            "v2_plane": 16 * KIB, "wv_scales_raw": 18 * KIB, "road_second": 18 * KIB, "wo_raw": 18 * KIB,
-            "road_scales": 34 * KIB, "wg_second": 34 * KIB,
+            "road_first": 0, "ws_raw": 0, "sensor_words": 8 * KIB, "v2_plane": 16 * KIB,
+            "warm_out": 17 * KIB - 64, "wg_second": 17 * KIB, "wo_raw": 17 * KIB,
+            "road_scales": 25 * KIB, "road_second": 25 * KIB,
         }
 
         def late_tile(name, shape, dtype):
@@ -61,16 +60,17 @@ def tile_list_traffic_gated_forecast_kernel(
         road_scales = late_tile("road_scales", [P, T // 4], I32)
         sensor_scales = held("sensor_scales", [P, T2 // 4], I32)
         wv_planes = held("wv_planes", [P, 2, H // 4], I32)
-        second_plane = held("second_plane", [P, S // 4], I32)
+        road_planes = held("road_planes", [P, 2, S // 4], I32)
         identity = held("identity", [P, P], F32)
         warm_in = held("warm_in", [P, 1], F32)
-        warm_out = late_tile("warm_out", [P, 1], F32)
+        warm_out = late_tile("warm_out", [P, 32], F32)
 
         nc.gpsimd.memset(road_scales[:, T // 8 : T // 4], 0)
         nc.vector.memset(road_scales[:, 0 : T // 8], 0)
+        nc.vector.memset(sensor_scales[:], 0)
         nc.vector.memset(warm_in[:], 0.0)
         nc.vector.memset(wv_planes[:], 0)
-        nc.vector.memset(second_plane[96:P, :], 0)
+        nc.vector.memset(road_planes[:], 0)
 
         def load_words(tile, words):
             nc.sync.dma_start(out=tile, in_=words.rearrange("p t i -> p (t i)").bitcast(I32))
@@ -89,7 +89,7 @@ def tile_list_traffic_gated_forecast_kernel(
         nc.gpsimd.dma_start(out=bias_rows[BIAS_ROW + PACK : P, :], in_=bo.rearrange("(c p) -> c p", p=P))
 
         make_identity(nc, identity[:])
-        wv_scales_raw = late_tile("wv_scales_raw", [P, 2, H // 4], I32)
+        wv_scales_raw = held("wv_scales_raw", [P, 2, H // 4], I32)
         for quad in range(4):
             nc.sync.dma_start(
                 out=wv_scales_raw[32 * quad : 32 * quad + 4, :, :],
@@ -100,13 +100,9 @@ def tile_list_traffic_gated_forecast_kernel(
         wv_raw = held("wv_raw", [P, 2, H // 2], I32)
         nc.sync.dma_start(out=wv_raw[:], in_=wv_words.rearrange("a p n -> p a n").bitcast(I32))
 
-        scale_rows = tab_scales.rearrange("a (quad r) t -> r quad a t", r=4)
-        for r in range(4):
-            nc.sync.dma_start(out=road_scales[r:P:SECOND_ROW, :], in_=scale_rows[r].bitcast(I32))
-        nc.scalar.activation(warm_out[:, 0:1], warm_in[:], ACT.Sigmoid)
-        road_first = late_tile("road_first", [P, T + S // 4], I32)
-        load_words(road_first[:, 0:T], tab_words[0])
-        nc.vector.memset(sensor_scales[:], 0)
+        nc.sync.dma_start(
+            out=road_scales[0:P:4, :], in_=tab_scales.rearrange("a q t -> q a t").bitcast(I32)
+        )
         for quad in range(4):
             first = 32 * quad + SENSOR_ROW
             nc.sync.dma_start(
@@ -114,14 +110,17 @@ def tile_list_traffic_gated_forecast_kernel(
                 in_=tab2_scales[0, 4 * quad : 4 * quad + 4, :].bitcast(I32),
             )
 
+        nc.scalar.activation(warm_out[:, 0:1], warm_in[:], ACT.Sigmoid)
+        road_first = late_tile("road_first", [P, T + S // 4], I32)
+        load_words(road_first[:, 0:T], tab_words[0])
+        wg_second = late_tile("wg_second", [P, PACK, H], F32)
+        load_weight(wg_second, wg[K_PASS:K, :])
         for quad in range(4):
             rows = slice(32 * quad, 32 * quad + 4)
             nc.vector.tensor_copy(
                 out=wv_planes[rows].rearrange("p a (t b w) -> p a t b w", t=PACK, w=2),
                 in_=wv_scales_raw[rows].rearrange("p a (b t w) -> p a t b w", t=PACK, w=2),
             )
-        road_second = late_tile("road_second", [P, T], I32)
-        load_words(road_second[:], tab_words[1])
 
         def gather(name, window, offsets, count, dtype, slot=""):
             words = count if dtype == U32 else count // 4
@@ -147,11 +146,12 @@ def tile_list_traffic_gated_forecast_kernel(
             return quantize(name, grouped[:].rearrange("p t m j -> p (t m j)"), H)
 
         packed_planes = gather("packed_planes", road_scales[:], road_list[:], S, U8)
-        nc.sync.dma_start(
-            out=second_plane[0:PLANE_ROWS, :], in_=packed_planes[SECOND_ROW : SECOND_ROW + PLANE_ROWS, :]
-        )
-        wg_second = late_tile("wg_second", [P, PACK, H], F32)
-        load_weight(wg_second, wg[K_PASS:K, :])
+        for quad in range(4):
+            nc.sync.dma_start(
+                out=road_planes[32 * quad : 32 * quad + 4], in_=packed_planes[32 * quad : 32 * quad + 32 : 4, :]
+            )
+        road_second = late_tile("road_second", [P, T], I32)
+        load_words(road_second[:], tab_words[1])
         wg_q = {}
         wg0_grouped = held("wg0_grouped", [P, PACK, P, PACK], BF16)
         for t in range(PACK):
@@ -177,21 +177,28 @@ def tile_list_traffic_gated_forecast_kernel(
         load_words(sensor_words[:], tab2_words[0])
         v2_plane = gather("v2_plane", sensor_scales[:], sensor_list[:], S, U8)
 
-        half_cols = LIST_COLS // 2
-        v_second = {}
-        for half in range(2):
-            offsets = road_list[:, half * half_cols : (half + 1) * half_cols]
-            v_second[half] = gather("v_second%d" % half, road_second[:], offsets, HALF, U32)
+        wg1_grouped = held("wg1_grouped", [P, PACK, P, PACK], BF16)
+        for t in range(PACK):
+            cast_slot("scalar", wg1_grouped[:, t], wg_second, t)
+        codes, scales = quantize_slots("wg1", wg1_grouped)
+        for t in range(PACK):
+            wg_q[1, t] = (codes[:, t * P : (t + 1) * P], scales[:, t * P : (t + 1) * P])
         wo_raw = late_tile("wo_raw", [P, PACK, N], F32)
         wo_rows = wo.rearrange("(b t q) n -> t b q n", t=PACK, q=8)
         for t in range(PACK):
             nc.sync.dma_start(out=wo_raw[:, t, :], in_=wo_rows[t])
 
+        half_cols = LIST_COLS // 2
+        v_second = {}
+        for half in range(2):
+            offsets = road_list[:, half * half_cols : (half + 1) * half_cols]
+            v_second[half] = gather("v_second%d" % half, road_second[:], offsets, HALF, U32)
+
         def road_operand(a, half):
             cols = slice(half * HALF, (half + 1) * HALF)
             if a == 0:
-                return v_first[:, cols].bitcast(FP8X4), packed_planes[:].bitcast(U8)[:, cols]
-            return v_second[half][:].bitcast(FP8X4), second_plane[:].bitcast(U8)[:, cols]
+                return v_first[:, cols].bitcast(FP8X4), road_planes[:, 0, :].bitcast(U8)[:, cols]
+            return v_second[half][:].bitcast(FP8X4), road_planes[:, 1, :].bitcast(U8)[:, cols]
 
         def gate_pass(bank, a, half, t, opens):
             codes, scales = wg_q[a, t]
@@ -218,17 +225,6 @@ def tile_list_traffic_gated_forecast_kernel(
         for t in range(PACK):
             value_banks[0, t] = bank_tile(PACK + t, [P, HALF])
             value_pass(value_banks[0, t], 0, 0, t)
-        for t in range(PACK):
-            value_pass(value_banks[0, t], 1, 0, t)
-
-        wg1_grouped = [held("wg1_grouped%d" % t, [P, P, PACK], BF16) for t in range(PACK)]
-        cast_slot("scalar", wg1_grouped[0][:], wg_second, 0)
-        for t in range(PACK):
-            if t + 1 < PACK:
-                cast_slot("scalar" if t == 0 else "vector", wg1_grouped[t + 1][:], wg_second, t + 1)
-            codes, scales = quantize("wg1_%d" % t, wg1_grouped[t][:].rearrange("p m j -> p (m j)"), P)
-            wg_q[1, t] = (codes[:], scales[:])
-
         gated = [held("gated%d" % half, [P, PACK, HALF], F32) for half in range(2)]
 
         def sigmoid_gate(half, t):
@@ -238,6 +234,7 @@ def tile_list_traffic_gated_forecast_kernel(
 
         for t in range(PACK):
             gate_pass(gate_banks[0, t], 1, 0, t, False)
+            value_pass(value_banks[0, t], 1, 0, t)
             nc.vector.tensor_tensor(gated[0][:, t, :], value_banks[0, t][:], sigmoid_gate(0, t)[:], ALU.mult)
 
         ws_grouped = held("ws_grouped", [P, PACK, P, PACK], BF16)
@@ -293,7 +290,12 @@ def tile_list_traffic_gated_forecast_kernel(
                 half, inside = divmod(start, HALF)
                 bank = sensor_banks[start]
                 h_part = h_grouped[:, start - first : start - first + CHUNK, :]
-                nc.vector.tensor_tensor(
+                if start == POOL_CHUNK:
+                    parked = held("parked_sensor", [P, PACK, CHUNK], F32)
+                    nc.scalar.copy(out=parked[:], in_=bank[:])
+                    bank = parked
+                engine = nc.gpsimd if start == POOL_CHUNK else nc.vector
+                engine.tensor_tensor(
                     h_part.rearrange("p (c i) t -> p c t i", i=2),
                     bank[:].rearrange("p t (c i) -> p c t i", i=2),
                     gated[half][:, :, inside : inside + CHUNK].rearrange("p t (c i) -> p c t i", i=2),
@@ -303,7 +305,7 @@ def tile_list_traffic_gated_forecast_kernel(
             result = held("result%d" % first, [P, N // P, width], F32)
             for c in range(N // P):
                 cols = slice(c * P, (c + 1) * P)
-                bank = bank_tile((6, 7, 4, 2, 5, 3, 0, 1)[2 * group + c], [P, width])
+                bank = bank_tile((6, 7, 4, 2, 6, 7, 5, 4, 2, 3, 6, 7)[2 * group + c], [P, width])
                 nc.tensor.matmul_mx(
                     out=bank[:], lhsT=wo_codes[:, cols].bitcast(FP8X4), lhsT_scale=wo_scales[:, cols],
                     rhs=codes[:].bitcast(FP8X4), rhs_scale=scales[:], start=True, stop=True,

@@ -164,12 +164,6 @@ def tile_list_traffic_gated_forecast_kernel(
         nc.tensor.transpose(bias_bank[:], bias_rows[:], identity[:])
         nc.scalar.copy(out=bias[:], in_=bias_bank[:, BIAS_ROW:P])
 
-        wv_codes = held("wv_codes", [P, 2, H // 2], I32)
-        for a in range(2):
-            nc.vector.tensor_copy(
-                out=wv_codes[:, a, :].rearrange("p (t b w) -> p t b w", t=PACK, w=4),
-                in_=wv_raw[:, a, :].rearrange("p (b t w) -> p t b w", t=PACK, w=4),
-            )
         v_first = gather("v_first", road_first[:, 0:T], road_list[:], S, U32)
         ws_raw = late_tile("ws_raw", [P, PACK, H], F32)
         load_weight(ws_raw, ws)
@@ -183,6 +177,12 @@ def tile_list_traffic_gated_forecast_kernel(
         codes, scales = quantize_slots("wg1", wg1_grouped)
         for t in range(PACK):
             wg_q[1, t] = (codes[:, t * P : (t + 1) * P], scales[:, t * P : (t + 1) * P])
+        wv_codes = held("wv_codes", [P, 2, H // 2], I32, "sensor_scales")
+        for a in range(2):
+            nc.vector.tensor_copy(
+                out=wv_codes[:, a, :].rearrange("p (t b w) -> p t b w", t=PACK, w=4),
+                in_=wv_raw[:, a, :].rearrange("p (b t w) -> p t b w", t=PACK, w=4),
+            )
         wo_raw = late_tile("wo_raw", [P, PACK, N], F32)
         wo_rows = wo.rearrange("(b t q) n -> t b q n", t=PACK, q=8)
         for t in range(PACK):

@@ -27,6 +27,7 @@ POOL_CHUNK = 896
 LIST_COLS = S // 16
 SENSOR_ROW = 8
 BIAS_ROW = 122
+SPREAD_WORDS = S // 4 + H // 4
 
 
 def tile_list_traffic_gated_forecast_kernel(
@@ -49,7 +50,7 @@ def tile_list_traffic_gated_forecast_kernel(
         late_offset = {
             "road_first": 0, "ws_raw": 0, "sensor_words": 8 * KIB, "v2_plane": 16 * KIB,
             "warm_out": 17 * KIB - 64, "wg_second": 17 * KIB, "wo_raw": 17 * KIB,
-            "road_scales": 25 * KIB, "road_second": 25 * KIB,
+            "packed_planes": 25 * KIB, "road_second": 25 * KIB,
         }
 
         def late_tile(name, shape, dtype):
@@ -57,10 +58,11 @@ def tile_list_traffic_gated_forecast_kernel(
 
         road_list = keep.tile([P, LIST_COLS], U16, name="road_list")
         sensor_list = keep.tile([P, LIST_COLS], U16, name="sensor_list")
-        road_scales = late_tile("road_scales", [P, T // 4], I32)
+        road_scales = held("road_scales", [P, T // 4], I32)
         sensor_scales = held("sensor_scales", [P, T2 // 4], I32)
         wv_planes = held("wv_planes", [P, 2, H // 4], I32)
-        road_planes = held("road_planes", [P, 2, S // 4], I32)
+        road_planes = held("road_planes", [P, 2, SPREAD_WORDS], I32)
+        sensor_plane = held("sensor_plane", [P, S // 4], I32)
         identity = held("identity", [P, P], F32)
         warm_in = held("warm_in", [P, 1], F32)
         warm_out = late_tile("warm_out", [P, 32], F32)
@@ -69,8 +71,8 @@ def tile_list_traffic_gated_forecast_kernel(
         nc.vector.memset(road_scales[:, 0 : T // 8], 0)
         nc.vector.memset(sensor_scales[:], 0)
         nc.vector.memset(warm_in[:], 0.0)
-        nc.vector.memset(wv_planes[:], 0)
         nc.vector.memset(road_planes[:], 0)
+        nc.vector.memset(sensor_plane[:], 0)
 
         def load_words(tile, words):
             nc.sync.dma_start(out=tile, in_=words.rearrange("p t i -> p (t i)").bitcast(I32))
@@ -89,12 +91,10 @@ def tile_list_traffic_gated_forecast_kernel(
         nc.gpsimd.dma_start(out=bias_rows[BIAS_ROW + PACK : P, :], in_=bo.rearrange("(c p) -> c p", p=P))
 
         make_identity(nc, identity[:])
-        wv_scales_raw = held("wv_scales_raw", [P, 2, H // 4], I32)
-        for quad in range(4):
-            nc.sync.dma_start(
-                out=wv_scales_raw[32 * quad : 32 * quad + 4, :, :],
-                in_=wv_scales[:, 4 * quad : 4 * quad + 4, :].rearrange("a r n -> r a n").bitcast(I32),
-            )
+        spread = held("spread", [P, SPREAD_WORDS], I32)
+        nc.sync.dma_start(
+            out=spread[0:P:4, S // 4 : SPREAD_WORDS], in_=wv_scales.rearrange("a q n -> q a n").bitcast(I32)
+        )
         wg_first = held("wg_first", [P, PACK, H], F32)
         load_weight(wg_first, wg[0:K_PASS, :])
         wv_raw = held("wv_raw", [P, 2, H // 2], I32)
@@ -103,24 +103,12 @@ def tile_list_traffic_gated_forecast_kernel(
         nc.sync.dma_start(
             out=road_scales[0:P:4, :], in_=tab_scales.rearrange("a q t -> q a t").bitcast(I32)
         )
-        for quad in range(4):
-            first = 32 * quad + SENSOR_ROW
-            nc.sync.dma_start(
-                out=sensor_scales[first : first + 4, :],
-                in_=tab2_scales[0, 4 * quad : 4 * quad + 4, :].bitcast(I32),
-            )
-
+        nc.sync.dma_start(out=sensor_scales[0:P:8, :], in_=tab2_scales[0].bitcast(I32))
         nc.scalar.activation(warm_out[:, 0:1], warm_in[:], ACT.Sigmoid)
         road_first = late_tile("road_first", [P, T + S // 4], I32)
         load_words(road_first[:, 0:T], tab_words[0])
         wg_second = late_tile("wg_second", [P, PACK, H], F32)
         load_weight(wg_second, wg[K_PASS:K, :])
-        for quad in range(4):
-            rows = slice(32 * quad, 32 * quad + 4)
-            nc.vector.tensor_copy(
-                out=wv_planes[rows].rearrange("p a (t b w) -> p a t b w", t=PACK, w=2),
-                in_=wv_scales_raw[rows].rearrange("p a (b t w) -> p a t b w", t=PACK, w=2),
-            )
 
         def gather(name, window, offsets, count, dtype, slot=""):
             words = count if dtype == U32 else count // 4
@@ -146,9 +134,10 @@ def tile_list_traffic_gated_forecast_kernel(
             return quantize(name, grouped[:].rearrange("p t m j -> p (t m j)"), H)
 
         packed_planes = gather("packed_planes", road_scales[:], road_list[:], S, U8)
+        nc.vector.tensor_copy(out=spread[:, 0 : S // 4], in_=packed_planes[:])
         for quad in range(4):
             nc.sync.dma_start(
-                out=road_planes[32 * quad : 32 * quad + 4], in_=packed_planes[32 * quad : 32 * quad + 32 : 4, :]
+                out=road_planes[32 * quad : 32 * quad + 4], in_=spread[32 * quad : 32 * quad + 32 : 4, :]
             )
         road_second = late_tile("road_second", [P, T], I32)
         load_words(road_second[:], tab_words[1])
@@ -170,6 +159,9 @@ def tile_list_traffic_gated_forecast_kernel(
         sensor_words = late_tile("sensor_words", [P, T2], I32)
         load_words(sensor_words[:], tab2_words[0])
         v2_plane = gather("v2_plane", sensor_scales[:], sensor_list[:], S, U8)
+        for quad in range(4):
+            first = 32 * quad + SENSOR_ROW
+            nc.sync.dma_start(out=sensor_plane[first : first + 4, :], in_=v2_plane[32 * quad : 32 * quad + 32 : 8, :])
 
         wg1_grouped = held("wg1_grouped", [P, PACK, P, PACK], BF16)
         for t in range(PACK):
@@ -183,6 +175,10 @@ def tile_list_traffic_gated_forecast_kernel(
                 out=wv_codes[:, a, :].rearrange("p (t b w) -> p t b w", t=PACK, w=4),
                 in_=wv_raw[:, a, :].rearrange("p (b t w) -> p t b w", t=PACK, w=4),
             )
+        nc.vector.tensor_copy(
+            out=wv_planes[:].rearrange("p a (t b w) -> p a t b w", t=PACK, w=2),
+            in_=road_planes[:, :, S // 4 : SPREAD_WORDS].rearrange("p a (b t w) -> p a t b w", t=PACK, w=2),
+        )
         wo_raw = late_tile("wo_raw", [P, PACK, N], F32)
         wo_rows = wo.rearrange("(b t q) n -> t b q n", t=PACK, q=8)
         for t in range(PACK):
@@ -197,8 +193,8 @@ def tile_list_traffic_gated_forecast_kernel(
         def road_operand(a, half):
             cols = slice(half * HALF, (half + 1) * HALF)
             if a == 0:
-                return v_first[:, cols].bitcast(FP8X4), road_planes[:, 0, :].bitcast(U8)[:, cols]
-            return v_second[half][:].bitcast(FP8X4), road_planes[:, 1, :].bitcast(U8)[:, cols]
+                return v_first[:, cols].bitcast(FP8X4), road_planes[:, 0, 0 : S // 4].bitcast(U8)[:, cols]
+            return v_second[half][:].bitcast(FP8X4), road_planes[:, 1, 0 : S // 4].bitcast(U8)[:, cols]
 
         def gate_pass(bank, a, half, t, opens):
             codes, scales = wg_q[a, t]
@@ -271,7 +267,7 @@ def tile_list_traffic_gated_forecast_kernel(
                     out=bank[:, t, :], lhsT=ws_codes[:, cols].bitcast(FP8X4),
                     lhsT_scale=ws_scales[:, cols],
                     rhs=v2[half][:, inside : inside + CHUNK].bitcast(FP8X4),
-                    rhs_scale=v2_plane[:].bitcast(U8)[SENSOR_ROW:P, start : start + CHUNK],
+                    rhs_scale=sensor_plane[:].bitcast(U8)[SENSOR_ROW:P, start : start + CHUNK],
                     start=True, stop=True,
                 )
             sensor_banks[start] = bank

@@ -1,7 +1,6 @@
 from contextlib import ExitStack
 
 import concourse.mybir as mybir
-from concourse.masks import make_identity
 
 K, K2, H, N, T, T2, S = 1024, 512, 512, 256, 4096, 2048, 1024
 FLOPS = 2 * S * (2 * K * H + K2 * H + H * N)
@@ -49,7 +48,7 @@ def tile_list_traffic_gated_forecast_kernel(
         KIB = 1024
         late_offset = {
             "road_first": 0, "ws_raw": 0, "sensor_words": 8 * KIB, "v2_plane": 16 * KIB,
-            "warm_out": 17 * KIB - 64, "wg_second": 17 * KIB, "wo_raw": 17 * KIB,
+            "zeros": 17 * KIB - 256, "wg_second": 17 * KIB, "wo_raw": 17 * KIB,
             "packed_planes": 25 * KIB, "road_second": 25 * KIB,
         }
 
@@ -64,13 +63,18 @@ def tile_list_traffic_gated_forecast_kernel(
         road_planes = held("road_planes", [P, 2, SPREAD_WORDS], I32)
         sensor_plane = held("sensor_plane", [P, S // 4], I32)
         identity = held("identity", [P, P], F32)
-        warm_in = held("warm_in", [P, 1], F32)
-        warm_out = late_tile("warm_out", [P, 32], F32)
+        zeros = late_tile("zeros", [P, P], F32)
+        bias_rows = held("bias_rows", [P, P], F32)
 
         nc.gpsimd.memset(road_scales[:, T // 8 : T // 4], 0)
         nc.vector.memset(road_scales[:, 0 : T // 8], 0)
         nc.vector.memset(sensor_scales[:], 0)
-        nc.vector.memset(warm_in[:], 0.0)
+        nc.vector.memset(zeros[:], 0.0)
+        nc.vector.memset(bias_rows[:], 0.0)
+        nc.gpsimd.affine_select(
+            out=identity[:], in_=zeros[:], pattern=[[-1, P]], compare_op=ALU.not_equal, fill=1.0,
+            base=0, channel_multiplier=1,
+        )
         nc.vector.memset(road_planes[:], 0)
         nc.vector.memset(sensor_plane[:], 0)
 
@@ -82,15 +86,12 @@ def tile_list_traffic_gated_forecast_kernel(
 
         nc.sync.dma_start(road_list[:], offs)
         nc.sync.dma_start(sensor_list[:], offs2)
-        bias_rows = held("bias_rows", [P, P], F32)
-        nc.vector.memset(bias_rows[0:BIAS_ROW, :], 0.0)
         nc.gpsimd.dma_start(
             out=bias_rows[BIAS_ROW : BIAS_ROW + PACK, :],
             in_=bg.rearrange("(b t q) -> t b q", t=PACK, q=8),
         )
         nc.gpsimd.dma_start(out=bias_rows[BIAS_ROW + PACK : P, :], in_=bo.rearrange("(c p) -> c p", p=P))
 
-        make_identity(nc, identity[:])
         spread = held("spread", [P, SPREAD_WORDS], I32)
         nc.sync.dma_start(
             out=spread[0:P:4, S // 4 : SPREAD_WORDS], in_=wv_scales.rearrange("a q n -> q a n").bitcast(I32)
@@ -104,7 +105,6 @@ def tile_list_traffic_gated_forecast_kernel(
             out=road_scales[0:P:4, :], in_=tab_scales.rearrange("a q t -> q a t").bitcast(I32)
         )
         nc.sync.dma_start(out=sensor_scales[0:P:8, :], in_=tab2_scales[0].bitcast(I32))
-        nc.scalar.activation(warm_out[:, 0:1], warm_in[:], ACT.Sigmoid)
         road_first = late_tile("road_first", [P, T + S // 4], I32)
         load_words(road_first[:, 0:T], tab_words[0])
         wg_second = late_tile("wg_second", [P, PACK, H], F32)

@@ -70,6 +70,8 @@ def tile_list_traffic_gated_forecast_kernel(
         nc.vector.memset(road_scales[:, 0 : T // 8], 0)
         nc.vector.memset(sensor_scales[:], 0)
         nc.vector.memset(zeros[:], 0.0)
+        warm = held("warm", [P, 1], F32)
+        nc.scalar.activation(warm[:], zeros[:, 0:1], ACT.Sigmoid)
         nc.vector.memset(bias_rows[:], 0.0)
         nc.gpsimd.affine_select(
             out=identity[:], in_=zeros[:], pattern=[[-1, P]], compare_op=ALU.not_equal, fill=1.0,

@@ -21,12 +21,26 @@ PACK = 4
 K_PASS = P * PACK
 HALF = 512
 CHUNK = 128
-OUT_GROUPS = ((0, 256), (256, 256), (512, 128), (640, 128), (768, 128), (896, 128))
-POOL_CHUNK = 896
+PARKED, DIRECT = 0, 1
+OUT_GROUPS = ((512, 256), (768, 256), (0, 256), (256, 128), (384, 128))
+POOL_CHUNKS = (384,)
+SENSOR_PIECES = ((512, 256), (768, 256), (0, 512))
 LIST_COLS = S // 16
+ROAD_ROW = P - 32
+SENSOR_LOAD_ROW = P - 16
 SENSOR_ROW = 8
-BIAS_ROW = 122
-SPREAD_WORDS = S // 4 + H // 4
+BIAS_ROW = P - 6
+ROAD_WORDS = S // 4
+PLANE_WORDS = ROAD_WORDS + H // 4
+KIB = 1024
+REUSED = {
+    "road_first": 0, "wg_second": 0, "ws_raw": 8 * KIB,
+    "wg_first": 16 * KIB, "wo_raw": 16 * KIB, "packed_planes": 24 * KIB - 512,
+    "road_second": 24 * KIB, "sensor_words": 32 * KIB,
+    "road_scales": 40 * KIB, "sensor_picked": 40 * KIB,
+    "sensor_plane": 26 * KIB, "wg0_grouped0": 28 * KIB, "wg0_grouped1": 30 * KIB,
+        "wv_codes": 44 * KIB, "wg1_grouped2": 44 * KIB, "wg1_grouped3": 45 * KIB,
+}
 
 
 def tile_list_traffic_gated_forecast_kernel(
@@ -36,193 +50,181 @@ def tile_list_traffic_gated_forecast_kernel(
     nc = tc.nc
     with ExitStack() as ctx:
         keep = ctx.enter_context(tc.tile_pool(name="keep", bufs=1))
-        late = ctx.enter_context(tc.tile_pool(name="late", bufs=1))
+        reused = ctx.enter_context(tc.tile_pool(name="reused", bufs=1))
         psum = ctx.enter_context(tc.psum_pool(name="psum", bufs=1))
 
         def bank_tile(index, shape):
             return psum.tile(shape, F32, name="bank%d" % index)
 
-        def held(name, shape, dtype, slot=""):
-            return keep.tile(shape, dtype, name=name, tag=slot or name, align_bytes=64)
+        def held(name, shape, dtype):
+            if name in REUSED:
+                return reused.tile(shape, dtype, name=name, align_bytes=64, offset=REUSED[name])
+            return keep.tile(shape, dtype, name=name, align_bytes=64)
 
-        KIB = 1024
-        late_offset = {
-            "road_first": 0, "ws_raw": 0, "sensor_words": 8 * KIB, "v2_plane": 16 * KIB,
-            "zeros": 17 * KIB - 256, "wg_second": 17 * KIB, "wo_raw": 17 * KIB,
-            "packed_planes": 25 * KIB, "road_second": 25 * KIB,
-        }
+        def load_words(name, words, columns):
+            table = held(name, [P, columns], I32)
+            nc.sync.dma_start(out=table[:], in_=words.rearrange("p t i -> p (t i)").bitcast(I32))
+            return table
 
-        def late_tile(name, shape, dtype):
-            return late.tile(shape, dtype, name=name, align_bytes=64, offset=late_offset[name])
+        def load_weight(name, rows):
+            raw = held(name, [P, PACK, H], F32)
+            nc.sync.dma_start(out=raw[:], in_=rows.rearrange("(p j) c -> p j c", j=PACK))
+            return raw
+
+        def gather(name, window, offsets, count, dtype):
+            picked = held(name, [P, count if dtype == U32 else count // 4], I32)
+            nc.vector.tensor_copy(picked[:].bitcast(dtype), window[:].bitcast(dtype).indirect(offsets))
+            return picked
+
+        def gather_half(name, window, index_list, half):
+            columns = LIST_COLS // 2
+            return gather(name, window, index_list[:, half * columns : (half + 1) * columns], HALF, U32)
+
+        def quantize(name, grouped, width):
+            codes = held(name + "_codes", [P, width], U32)
+            scales = held(name + "_scales", [P, width], U8)
+            nc.vector.quantize_mx(out=codes[:].bitcast(FP8X4), scales=scales[:], in_=grouped)
+            return codes, scales
+
+        def slot_views(grouped, raw, t):
+            source = raw[:].rearrange("p j (b t u i) -> p t b u j i", t=PACK, u=4, i=2)
+            return grouped.rearrange("p (b u i) j -> p b u j i", u=4, i=2), source[:, t]
 
         road_list = keep.tile([P, LIST_COLS], U16, name="road_list")
         sensor_list = keep.tile([P, LIST_COLS], U16, name="sensor_list")
         road_scales = held("road_scales", [P, T // 4], I32)
         sensor_scales = held("sensor_scales", [P, T2 // 4], I32)
-        wv_planes = held("wv_planes", [P, 2, H // 4], I32)
-        road_planes = held("road_planes", [P, 2, SPREAD_WORDS], I32)
-        sensor_plane = held("sensor_plane", [P, S // 4], I32)
+        wv_scale_rows = held("wv_scale_rows", [P, H // 4], I32)
+        wv_raw = held("wv_raw", [P, 2, H // 2], I32)
+        planes = held("planes", [P, 2, PLANE_WORDS], I32)
+        zeros = held("zeros", [P, P], F32)
         identity = held("identity", [P, P], F32)
-        zeros = late_tile("zeros", [P, P], F32)
         bias_rows = held("bias_rows", [P, P], F32)
 
-        nc.gpsimd.memset(road_scales[:, T // 8 : T // 4], 0)
-        nc.vector.memset(road_scales[:, 0 : T // 8], 0)
-        nc.vector.memset(sensor_scales[:], 0)
+        nc.sync.dma_start(road_list[:], offs)
+        nc.sync.dma_start(out=road_scales[ROAD_ROW:P, :], in_=tab_scales.rearrange("a q t -> q a t").bitcast(I32))
+        nc.sync.dma_start(out=wv_scale_rows[ROAD_ROW:P, :], in_=wv_scales.rearrange("a q n -> q a n").bitcast(I32))
+        nc.sync.dma_start(sensor_list[:], offs2)
+        nc.sync.dma_start(out=sensor_scales[SENSOR_LOAD_ROW:P, :], in_=tab2_scales[0].bitcast(I32))
+        nc.sync.dma_start(out=wv_raw[:], in_=wv_words.rearrange("a p n -> p a n").bitcast(I32))
+        road_first = load_words("road_first", tab_words[0], T)
+
         nc.vector.memset(zeros[:], 0.0)
         warm = held("warm", [P, 1], F32)
         nc.scalar.activation(warm[:], zeros[:, 0:1], ACT.Sigmoid)
-        nc.vector.memset(bias_rows[:], 0.0)
+        nc.vector.memset(road_scales[0:ROAD_ROW, :], 0)
+        nc.vector.memset(sensor_scales[0:SENSOR_LOAD_ROW, :], 0)
+        nc.vector.memset(bias_rows[0:BIAS_ROW, :], 0.0)
+        nc.gpsimd.memset(planes[:], 0)
         nc.gpsimd.affine_select(
             out=identity[:], in_=zeros[:], pattern=[[-1, P]], compare_op=ALU.not_equal, fill=1.0,
             base=0, channel_multiplier=1,
         )
-        nc.vector.memset(road_planes[:], 0)
-        nc.vector.memset(sensor_plane[:], 0)
-
-        def load_words(tile, words):
-            nc.sync.dma_start(out=tile, in_=words.rearrange("p t i -> p (t i)").bitcast(I32))
-
-        def load_weight(tile, rows):
-            nc.sync.dma_start(out=tile[:], in_=rows.rearrange("(p j) c -> p j c", j=PACK))
-
-        nc.sync.dma_start(road_list[:], offs)
-        nc.sync.dma_start(sensor_list[:], offs2)
         nc.gpsimd.dma_start(
-            out=bias_rows[BIAS_ROW : BIAS_ROW + PACK, :],
-            in_=bg.rearrange("(b t q) -> t b q", t=PACK, q=8),
+            out=bias_rows[BIAS_ROW : BIAS_ROW + PACK, :], in_=bg.rearrange("(b t q) -> t b q", t=PACK, q=8)
         )
         nc.gpsimd.dma_start(out=bias_rows[BIAS_ROW + PACK : P, :], in_=bo.rearrange("(c p) -> c p", p=P))
-
-        spread = held("spread", [P, SPREAD_WORDS], I32)
-        nc.sync.dma_start(
-            out=spread[0:P:4, S // 4 : SPREAD_WORDS], in_=wv_scales.rearrange("a q n -> q a n").bitcast(I32)
-        )
-        wg_first = held("wg_first", [P, PACK, H], F32)
-        load_weight(wg_first, wg[0:K_PASS, :])
-        wv_raw = held("wv_raw", [P, 2, H // 2], I32)
-        nc.sync.dma_start(out=wv_raw[:], in_=wv_words.rearrange("a p n -> p a n").bitcast(I32))
-
-        nc.sync.dma_start(
-            out=road_scales[0:P:4, :], in_=tab_scales.rearrange("a q t -> q a t").bitcast(I32)
-        )
-        nc.sync.dma_start(out=sensor_scales[0:P:8, :], in_=tab2_scales[0].bitcast(I32))
-        road_first = late_tile("road_first", [P, T + S // 4], I32)
-        load_words(road_first[:, 0:T], tab_words[0])
-        wg_second = late_tile("wg_second", [P, PACK, H], F32)
-        load_weight(wg_second, wg[K_PASS:K, :])
-
-        def gather(name, window, offsets, count, dtype, slot=""):
-            words = count if dtype == U32 else count // 4
-            picked = late_tile(name, [P, words], I32) if name in late_offset else held(name, [P, words], I32)
-            nc.vector.tensor_copy(picked[:].bitcast(dtype), window.bitcast(dtype).indirect(offsets))
-            return picked
-
-        def quantize(name, grouped, width, slot=""):
-            codes = held(name + "_codes", [P, width], U32, slot)
-            scales = held(name + "_scales", [P, width], U8)
-            nc.vector.quantize_mx(out=codes[:].bitcast(FP8X4), scales=scales[:], in_=grouped)
-            return codes, scales
-
-        def cast_slot(engine, grouped, raw, t):
-            source = raw[:].rearrange("p j (b t u i) -> p t b u j i", t=PACK, u=4, i=2)
-            target = grouped.rearrange("p (b u i) j -> p b u j i", u=4, i=2)
-            if engine == "scalar":
-                nc.scalar.copy(out=target, in_=source[:, t])
-            else:
-                nc.vector.tensor_copy(out=target, in_=source[:, t])
-
-        def quantize_slots(name, grouped):
-            return quantize(name, grouped[:].rearrange("p t m j -> p (t m j)"), H)
-
-        packed_planes = gather("packed_planes", road_scales[:], road_list[:], S, U8)
-        nc.vector.tensor_copy(out=spread[:, 0 : S // 4], in_=packed_planes[:])
-        for quad in range(4):
-            nc.sync.dma_start(
-                out=road_planes[32 * quad : 32 * quad + 4], in_=spread[32 * quad : 32 * quad + 32 : 4, :]
-            )
-        road_second = late_tile("road_second", [P, T], I32)
-        load_words(road_second[:], tab_words[1])
-        wg_q = {}
-        wg0_grouped = held("wg0_grouped", [P, PACK, P, PACK], BF16)
-        for t in range(PACK):
-            cast_slot("scalar", wg0_grouped[:, t], wg_first, t)
-        codes, scales = quantize_slots("wg0", wg0_grouped)
-        for t in range(PACK):
-            wg_q[0, t] = (codes[:, t * P : (t + 1) * P], scales[:, t * P : (t + 1) * P])
-        bias = held("bias", [P, P - BIAS_ROW], F32, "wg_first")
+        bias = held("bias", [P, P - BIAS_ROW], F32)
         bias_bank = bank_tile(7, [P, P])
         nc.tensor.transpose(bias_bank[:], bias_rows[:], identity[:])
         nc.scalar.copy(out=bias[:], in_=bias_bank[:, BIAS_ROW:P])
 
-        v_first = gather("v_first", road_first[:, 0:T], road_list[:], S, U32)
-        ws_raw = late_tile("ws_raw", [P, PACK, H], F32)
-        load_weight(ws_raw, ws)
-        sensor_words = late_tile("sensor_words", [P, T2], I32)
-        load_words(sensor_words[:], tab2_words[0])
-        v2_plane = gather("v2_plane", sensor_scales[:], sensor_list[:], S, U8)
+        packed_planes = gather("packed_planes", road_scales, road_list[:], S, U8)
+        staged = held("staged", [P, PLANE_WORDS], I32)
+        nc.vector.tensor_copy(
+            out=staged[ROAD_ROW:P, ROAD_WORDS:PLANE_WORDS].rearrange("p (t b w) -> p t b w", t=PACK, w=2),
+            in_=wv_scale_rows[ROAD_ROW:P, :].rearrange("p (b t w) -> p t b w", t=PACK, w=2),
+        )
+        nc.vector.tensor_copy(out=staged[ROAD_ROW:P, 0:ROAD_WORDS], in_=packed_planes[ROAD_ROW:P, :])
         for quad in range(4):
-            first = 32 * quad + SENSOR_ROW
-            nc.sync.dma_start(out=sensor_plane[first : first + 4, :], in_=v2_plane[32 * quad : 32 * quad + 32 : 8, :])
+            first = ROAD_ROW + 8 * quad
+            nc.sync.dma_start(out=planes[32 * quad : 32 * quad + 4], in_=staged[first : first + 8, :])
+        road_second = load_words("road_second", tab_words[1], T)
+        wg_first = load_weight("wg_first", wg[0:K_PASS, :])
 
-        wg1_grouped = held("wg1_grouped", [P, PACK, P, PACK], BF16)
-        for t in range(PACK):
-            cast_slot("scalar", wg1_grouped[:, t], wg_second, t)
-        codes, scales = quantize_slots("wg1", wg1_grouped)
-        for t in range(PACK):
-            wg_q[1, t] = (codes[:, t * P : (t + 1) * P], scales[:, t * P : (t + 1) * P])
-        wv_codes = held("wv_codes", [P, 2, H // 2], I32, "sensor_scales")
+        wv_codes = held("wv_codes", [P, 2, H // 2], I32)
         for a in range(2):
             nc.vector.tensor_copy(
                 out=wv_codes[:, a, :].rearrange("p (t b w) -> p t b w", t=PACK, w=4),
                 in_=wv_raw[:, a, :].rearrange("p (b t w) -> p t b w", t=PACK, w=4),
             )
-        nc.vector.tensor_copy(
-            out=wv_planes[:].rearrange("p a (t b w) -> p a t b w", t=PACK, w=2),
-            in_=road_planes[:, :, S // 4 : SPREAD_WORDS].rearrange("p a (b t w) -> p a t b w", t=PACK, w=2),
-        )
-        wo_raw = late_tile("wo_raw", [P, PACK, N], F32)
-        wo_rows = wo.rearrange("(b t q) n -> t b q n", t=PACK, q=8)
-        for t in range(PACK):
-            nc.sync.dma_start(out=wo_raw[:, t, :], in_=wo_rows[t])
+        sensor_picked = gather("sensor_picked", sensor_scales, sensor_list[:], S, U8)
 
-        half_cols = LIST_COLS // 2
-        v_second = {}
-        for half in range(2):
-            offsets = road_list[:, half * half_cols : (half + 1) * half_cols]
-            v_second[half] = gather("v_second%d" % half, road_second[:], offsets, HALF, U32)
+        road = {}
+        for half in (PARKED, DIRECT):
+            road[0, half] = gather_half("road0_%d" % half, road_first, road_list, half)
+        wg_second = load_weight("wg_second", wg[K_PASS:K, :])
+        ws_raw = load_weight("ws_raw", ws)
 
         def road_operand(a, half):
             cols = slice(half * HALF, (half + 1) * HALF)
-            if a == 0:
-                return v_first[:, cols].bitcast(FP8X4), road_planes[:, 0, 0 : S // 4].bitcast(U8)[:, cols]
-            return v_second[half][:].bitcast(FP8X4), road_planes[:, 1, 0 : S // 4].bitcast(U8)[:, cols]
-
-        def gate_pass(bank, a, half, t, opens):
-            codes, scales = wg_q[a, t]
-            rhs, rhs_scale = road_operand(a, half)
-            nc.tensor.matmul_mx(
-                out=bank[:], lhsT=codes.bitcast(FP8X4), lhsT_scale=scales,
-                rhs=rhs, rhs_scale=rhs_scale, start=opens, stop=not opens,
-            )
+            return road[a, half][:].bitcast(FP8X4), planes[:, a, 0:ROAD_WORDS].bitcast(U8)[:, cols]
 
         def value_pass(bank, a, half, t):
             rhs, rhs_scale = road_operand(a, half)
             nc.tensor.matmul_mx(
                 out=bank[:],
                 lhsT=wv_codes[:, a, :].bitcast(U8)[:, 2 * t * P : 2 * (t + 1) * P].bitcast(FP4X4),
-                lhsT_scale=wv_planes[:, a, :].bitcast(U8)[:, t * P : (t + 1) * P],
+                lhsT_scale=planes[:, a, ROAD_WORDS:PLANE_WORDS].bitcast(U8)[:, t * P : (t + 1) * P],
                 rhs=rhs, rhs_scale=rhs_scale, start=(a == 0), stop=(a == 1),
             )
 
         value_banks = {}
+        for half in (PARKED, DIRECT):
+            for t in range(PACK):
+                value_banks[half, t] = bank_tile(PACK * half + t, [P, HALF])
+                value_pass(value_banks[half, t], 0, half, t)
+        parked = {}
+        for half in (PARKED, DIRECT):
+            road[1, half] = gather_half("road1_%d" % half, road_second, road_list, half)
+            for t in range(PACK):
+                value_pass(value_banks[half, t], 1, half, t)
+                if half == PARKED:
+                    parked[t] = held("parked%d" % t, [P, HALF], F32)
+                    nc.scalar.copy(out=parked[t][:], in_=value_banks[half, t][:])
+        sensor_words = load_words("sensor_words", tab2_words[0], T2)
+        sensor_plane = held("sensor_plane", [P, S // 4], I32)
+        nc.gpsimd.memset(sensor_plane[:], 0)
+        for quad in range(4):
+            row = 32 * quad + SENSOR_ROW
+            first = SENSOR_LOAD_ROW + 4 * quad
+            nc.sync.dma_start(out=sensor_plane[row : row + 4, :], in_=sensor_picked[first : first + 4, :])
+
+        wg_q = {}
+
+        def gate_pass(bank, a, half, t):
+            codes, scales = wg_q[a, t]
+            rhs, rhs_scale = road_operand(a, half)
+            nc.tensor.matmul_mx(
+                out=bank[:], lhsT=codes.bitcast(FP8X4), lhsT_scale=scales,
+                rhs=rhs, rhs_scale=rhs_scale, start=(a == 0), stop=(a == 1),
+            )
+
         gate_banks = {}
+        pairs = [held("wg0_grouped%d" % u, [P, 2, P, PACK], BF16) for u in range(2)]
         for t in range(PACK):
-            gate_banks[0, t] = bank_tile(t, [P, HALF])
-            gate_pass(gate_banks[0, t], 0, 0, t, True)
+            target, source = slot_views(pairs[t // 2][:, t % 2], wg_first, t)
+            nc.vector.tensor_copy(out=target, in_=source)
+        for u in range(2):
+            codes, scales = quantize("wg0_%d" % u, pairs[u][:].rearrange("p t m j -> p (t m j)"), 2 * P)
+            for e in range(2):
+                t = 2 * u + e
+                wg_q[0, t] = (codes[:, e * P : (e + 1) * P], scales[:, e * P : (e + 1) * P])
+                gate_banks[DIRECT, t] = bank_tile(t, [P, HALF])
+                gate_pass(gate_banks[DIRECT, t], 0, DIRECT, t)
+        wo_raw = held("wo_raw", [P, PACK, N], F32)
+        wo_rows = wo.rearrange("(b t q) n -> t b q n", t=PACK, q=8)
         for t in range(PACK):
-            value_banks[0, t] = bank_tile(PACK + t, [P, HALF])
-            value_pass(value_banks[0, t], 0, 0, t)
+            nc.sync.dma_start(out=wo_raw[:, t, :], in_=wo_rows[t])
+
+        slots = [held("wg1_grouped%d" % t, [P, P, PACK], BF16) for t in range(PACK)]
+        for t in range(PACK):
+            target, source = slot_views(slots[t][:], wg_second, t)
+            if t < 2:
+                nc.vector.tensor_copy(out=target, in_=source)
+            else:
+                nc.scalar.copy(out=target, in_=source)
+
         gated = [held("gated%d" % half, [P, PACK, HALF], F32) for half in range(2)]
 
         def sigmoid_gate(half, t):
@@ -231,48 +233,50 @@ def tile_list_traffic_gated_forecast_kernel(
             return gate
 
         for t in range(PACK):
-            gate_pass(gate_banks[0, t], 1, 0, t, False)
-            value_pass(value_banks[0, t], 1, 0, t)
-            nc.vector.tensor_tensor(gated[0][:, t, :], value_banks[0, t][:], sigmoid_gate(0, t)[:], ALU.mult)
+            codes, scales = quantize("wg1_%d" % t, slots[t][:].rearrange("p m j -> p (m j)"), P)
+            wg_q[1, t] = (codes[:], scales[:])
+            gate_pass(gate_banks[DIRECT, t], 1, DIRECT, t)
+        for t in range(PACK):
+            nc.vector.tensor_tensor(
+                gated[DIRECT][:, t, :], value_banks[DIRECT, t][:], sigmoid_gate(DIRECT, t)[:], ALU.mult
+            )
 
         ws_grouped = held("ws_grouped", [P, PACK, P, PACK], BF16)
         ws_source = ws_raw[:].rearrange("p j (b t q) -> p t b q j", t=PACK, q=8)
-        for t in range(PACK):
+        for t in range(PACK - 1):
             nc.gpsimd.tensor_scalar(
                 ws_grouped[:, t].rearrange("p (b q) j -> p b q j", q=8), ws_source[:, t], 1.0, 0.0, ALU.mult, ALU.add
             )
+        target, source = slot_views(ws_grouped[:, PACK - 1], ws_raw, PACK - 1)
+        nc.scalar.copy(out=target, in_=source)
         for t in range(PACK):
-            value_banks[1, t] = bank_tile((0, 4, 5, 0)[t], [P, HALF])
+            gate_banks[PARKED, t] = bank_tile(t, [P, HALF])
             for a in range(2):
-                value_pass(value_banks[1, t], a, 1, t)
-            gate_banks[1, t] = bank_tile((1, 2, 3, 1)[t], [P, HALF])
-            for a in range(2):
-                gate_pass(gate_banks[1, t], a, 1, t, a == 0)
-            parked = held("parked%d" % t, [P, HALF], F32)
-            nc.scalar.copy(out=parked[:], in_=value_banks[1, t][:])
-            nc.gpsimd.tensor_tensor(gated[1][:, t, :], parked[:], sigmoid_gate(1, t)[:], ALU.mult)
+                gate_pass(gate_banks[PARKED, t], a, PARKED, t)
+            nc.gpsimd.tensor_tensor(gated[PARKED][:, t, :], parked[t][:], sigmoid_gate(PARKED, t)[:], ALU.mult)
 
-        v2 = []
-        for half in range(2):
-            offsets = sensor_list[:, half * half_cols : (half + 1) * half_cols]
-            v2.append(gather("v2_%d" % half, sensor_words[:], offsets, HALF, U32))
-            if half == 0:
-                ws_codes, ws_scales = quantize_slots("ws", ws_grouped)
+        ws_codes, ws_scales = quantize("ws", ws_grouped[:].rearrange("p t m j -> p (t m j)"), H)
+        sensor = {}
+        for first, count in SENSOR_PIECES:
+            offsets = sensor_list[:, first // 16 : (first + count) // 16]
+            picked = gather("sensor%d" % first, sensor_words, offsets, count, U32)
+            for start in range(first, first + count, CHUNK):
+                sensor[start] = picked[:, start - first : start - first + CHUNK]
 
         sensor_banks = {}
-        for start in range(0, S, CHUNK):
-            half, inside = divmod(start, HALF)
-            bank = bank_tile((6, 7, 4, 2, 5, 3, 0, 1)[start // CHUNK], [P, PACK, CHUNK])
-            for t in range(PACK):
-                cols = slice(t * P, (t + 1) * P)
-                nc.tensor.matmul_mx(
-                    out=bank[:, t, :], lhsT=ws_codes[:, cols].bitcast(FP8X4),
-                    lhsT_scale=ws_scales[:, cols],
-                    rhs=v2[half][:, inside : inside + CHUNK].bitcast(FP8X4),
-                    rhs_scale=sensor_plane[:].bitcast(U8)[SENSOR_ROW:P, start : start + CHUNK],
-                    start=True, stop=True,
-                )
-            sensor_banks[start] = bank
+        for half in (DIRECT, PARKED):
+            for inside in range(0, HALF, CHUNK):
+                start = half * HALF + inside
+                bank = bank_tile(start // CHUNK, [P, PACK, CHUNK])
+                for t in range(PACK):
+                    cols = slice(t * P, (t + 1) * P)
+                    nc.tensor.matmul_mx(
+                        out=bank[:, t, :], lhsT=ws_codes[:, cols].bitcast(FP8X4), lhsT_scale=ws_scales[:, cols],
+                        rhs=sensor[start].bitcast(FP8X4),
+                        rhs_scale=sensor_plane[:].bitcast(U8)[SENSOR_ROW:P, start : start + CHUNK],
+                        start=True, stop=True,
+                    )
+                sensor_banks[start] = bank
 
         wo_grouped = held("wo_grouped", [P, N, PACK], BF16)
         nc.scalar.copy(
@@ -288,11 +292,11 @@ def tile_list_traffic_gated_forecast_kernel(
                 half, inside = divmod(start, HALF)
                 bank = sensor_banks[start]
                 h_part = h_grouped[:, start - first : start - first + CHUNK, :]
-                if start == POOL_CHUNK:
-                    parked = held("parked_sensor", [P, PACK, CHUNK], F32)
-                    nc.scalar.copy(out=parked[:], in_=bank[:])
-                    bank = parked
-                engine = nc.gpsimd if start == POOL_CHUNK else nc.vector
+                engine = nc.vector
+                if start in POOL_CHUNKS:
+                    parked_sensor = held("parked_sensor%d" % start, [P, PACK, CHUNK], F32)
+                    nc.scalar.copy(out=parked_sensor[:], in_=bank[:])
+                    bank, engine = parked_sensor, nc.gpsimd
                 engine.tensor_tensor(
                     h_part.rearrange("p (c i) t -> p c t i", i=2),
                     bank[:].rearrange("p t (c i) -> p c t i", i=2),
@@ -303,13 +307,13 @@ def tile_list_traffic_gated_forecast_kernel(
             result = held("result%d" % first, [P, N // P, width], F32)
             for c in range(N // P):
                 cols = slice(c * P, (c + 1) * P)
-                bank = bank_tile((6, 7, 4, 2, 6, 7, 5, 4, 2, 3, 6, 7)[2 * group + c], [P, width])
+                bank = bank_tile((4, 5, 6, 7, 3, 0, 1, 4, 5, 6)[2 * group + c], [P, width])
                 nc.tensor.matmul_mx(
                     out=bank[:], lhsT=wo_codes[:, cols].bitcast(FP8X4), lhsT_scale=wo_scales[:, cols],
                     rhs=codes[:].bitcast(FP8X4), rhs_scale=scales[:], start=True, stop=True,
                 )
                 column = bias[:, PACK + c : PACK + c + 1]
-                if first + width == S and c == 1:
+                if group == len(OUT_GROUPS) - 1 and c == 1:
                     nc.vector.tensor_scalar(result[:, c, :], bank[:], column, None, ALU.add)
                 else:
                     nc.scalar.activation(result[:, c, :], bank[:], ACT.Identity, bias=column)

@@ -184,7 +184,6 @@ def tile_list_traffic_gated_forecast_kernel(
                     nc.scalar.copy(out=parked[t][:], in_=value_banks[half, t][:])
         sensor_words = load_words("sensor_words", tab2_words[0], T2)
         sensor_plane = held("sensor_plane", [P, S // 4], I32)
-        nc.gpsimd.memset(sensor_plane[:], 0)
         for quad in range(4):
             row = 32 * quad + SENSOR_ROW
             first = SENSOR_LOAD_ROW + 4 * quad
@@ -242,11 +241,11 @@ def tile_list_traffic_gated_forecast_kernel(
             )
 
         ws_grouped = held("ws_grouped", [P, PACK, P, PACK], BF16)
-        ws_source = ws_raw[:].rearrange("p j (b t q) -> p t b q j", t=PACK, q=8)
-        for t in range(PACK - 1):
-            nc.gpsimd.tensor_scalar(
-                ws_grouped[:, t].rearrange("p (b q) j -> p b q j", q=8), ws_source[:, t], 1.0, 0.0, ALU.mult, ALU.add
-            )
+        nc.gpsimd.tensor_scalar(
+            ws_grouped[:, 0 : PACK - 1].rearrange("p t (b q) j -> p b t (q j)", q=8),
+            ws_raw[:].rearrange("p j (b c) -> p b c j", c=32)[:, :, 0 : 8 * (PACK - 1), :],
+            1.0, 0.0, ALU.mult, ALU.add,
+        )
         target, source = slot_views(ws_grouped[:, PACK - 1], ws_raw, PACK - 1)
         nc.scalar.copy(out=target, in_=source)
         for t in range(PACK):

@@ -22,7 +22,7 @@ K_PASS = P * PACK
 HALF = 512
 CHUNK = 128
 PARKED, DIRECT = 0, 1
-OUT_GROUPS = ((512, 256), (768, 256), (0, 256), (256, 128), (384, 128))
+OUT_GROUPS = ((512, 256), (768, 256), (0, 256), (256, 256))
 POOL_CHUNKS = (384,)
 SENSOR_PIECES = ((512, 256), (768, 256), (0, 512))
 LIST_COLS = S // 16
@@ -37,9 +37,11 @@ REUSED = {
     "road_first": 0, "wg_second": 0, "ws_raw": 8 * KIB,
     "wg_first": 16 * KIB, "wo_raw": 16 * KIB, "packed_planes": 24 * KIB - 512,
     "road_second": 24 * KIB, "sensor_words": 32 * KIB,
-    "road_scales": 40 * KIB, "sensor_picked": 40 * KIB,
+    "road_scales": 40 * KIB, "planes": 40 * KIB, "sensor_picked": 43 * KIB,
     "sensor_plane": 26 * KIB, "wg0_grouped0": 28 * KIB, "wg0_grouped1": 30 * KIB,
-        "wv_codes": 44 * KIB, "wg1_grouped2": 44 * KIB, "wg1_grouped3": 45 * KIB,
+        "ws_grouped": 60 * KIB, "gated0": 60 * KIB,
+    "lead_grouped": 56 * KIB, "h_grouped256": 56 * KIB, "h_grouped0": 18 * KIB, "parked_sensor384": 16 * KIB,
+    "wv_codes": 44 * KIB, "wg1_grouped2": 44 * KIB, "wg1_grouped3": 45 * KIB,
 }
 
 
@@ -96,7 +98,6 @@ def tile_list_traffic_gated_forecast_kernel(
         sensor_scales = held("sensor_scales", [P, T2 // 4], I32)
         wv_scale_rows = held("wv_scale_rows", [P, H // 4], I32)
         wv_raw = held("wv_raw", [P, 2, H // 2], I32)
-        planes = held("planes", [P, 2, PLANE_WORDS], I32)
         zeros = held("zeros", [P, P], F32)
         identity = held("identity", [P, P], F32)
         bias_rows = held("bias_rows", [P, P], F32)
@@ -115,7 +116,6 @@ def tile_list_traffic_gated_forecast_kernel(
         nc.vector.memset(road_scales[0:ROAD_ROW, :], 0)
         nc.vector.memset(sensor_scales[0:SENSOR_LOAD_ROW, :], 0)
         nc.vector.memset(bias_rows[0:BIAS_ROW, :], 0.0)
-        nc.gpsimd.memset(planes[:], 0)
         nc.gpsimd.affine_select(
             out=identity[:], in_=zeros[:], pattern=[[-1, P]], compare_op=ALU.not_equal, fill=1.0,
             base=0, channel_multiplier=1,
@@ -136,6 +136,7 @@ def tile_list_traffic_gated_forecast_kernel(
             in_=wv_scale_rows[ROAD_ROW:P, :].rearrange("p (b t w) -> p t b w", t=PACK, w=2),
         )
         nc.vector.tensor_copy(out=staged[ROAD_ROW:P, 0:ROAD_WORDS], in_=packed_planes[ROAD_ROW:P, :])
+        planes = held("planes", [P, 2, PLANE_WORDS], I32)
         for quad in range(4):
             first = ROAD_ROW + 8 * quad
             nc.sync.dma_start(out=planes[32 * quad : 32 * quad + 4], in_=staged[first : first + 8, :])
@@ -224,7 +225,7 @@ def tile_list_traffic_gated_forecast_kernel(
             else:
                 nc.scalar.copy(out=target, in_=source)
 
-        gated = [held("gated%d" % half, [P, PACK, HALF], F32) for half in range(2)]
+        gated = {DIRECT: held("gated1", [P, PACK, HALF], F32)}
 
         def sigmoid_gate(half, t):
             gate = held("gate%d_%d" % (half, t), [P, HALF], F32)
@@ -248,13 +249,14 @@ def tile_list_traffic_gated_forecast_kernel(
         )
         target, source = slot_views(ws_grouped[:, PACK - 1], ws_raw, PACK - 1)
         nc.scalar.copy(out=target, in_=source)
+        ws_codes, ws_scales = quantize("ws", ws_grouped[:].rearrange("p t m j -> p (t m j)"), H)
+        gated[PARKED] = held("gated0", [P, PACK, HALF], F32)
         for t in range(PACK):
             gate_banks[PARKED, t] = bank_tile(t, [P, HALF])
             for a in range(2):
                 gate_pass(gate_banks[PARKED, t], a, PARKED, t)
             nc.gpsimd.tensor_tensor(gated[PARKED][:, t, :], parked[t][:], sigmoid_gate(PARKED, t)[:], ALU.mult)
 
-        ws_codes, ws_scales = quantize("ws", ws_grouped[:].rearrange("p t m j -> p (t m j)"), H)
         sensor = {}
         for first, count in SENSOR_PIECES:
             offsets = sensor_list[:, first // 16 : (first + count) // 16]
@@ -277,16 +279,18 @@ def tile_list_traffic_gated_forecast_kernel(
                     )
                 sensor_banks[start] = bank
 
-        wo_grouped = held("wo_grouped", [P, N, PACK], BF16)
+        lead_grouped = held("lead_grouped", [P, N + OUT_GROUPS[0][1], PACK], BF16)
         nc.scalar.copy(
-            out=wo_grouped[:].rearrange("p (c i) t -> p c t i", i=2),
+            out=lead_grouped[:, 0:N, :].rearrange("p (c i) t -> p c t i", i=2),
             in_=wo_raw[:].rearrange("p t (c i) -> p c t i", i=2),
         )
-        wo_codes, wo_scales = quantize("wo", wo_grouped[:].rearrange("p n t -> p (n t)"), N)
 
         out_rows = out.rearrange("(c p) j -> p c j", p=P)
         for group, (first, width) in enumerate(OUT_GROUPS):
-            h_grouped = held("h_grouped%d" % first, [P, width, PACK], BF16)
+            if group == 0:
+                h_grouped = lead_grouped[:, N : N + width, :]
+            else:
+                h_grouped = held("h_grouped%d" % first, [P, width, PACK], BF16)
             for start in range(first, first + width, CHUNK):
                 half, inside = divmod(start, HALF)
                 bank = sensor_banks[start]
@@ -302,11 +306,16 @@ def tile_list_traffic_gated_forecast_kernel(
                     gated[half][:, :, inside : inside + CHUNK].rearrange("p t (c i) -> p c t i", i=2),
                     ALU.add,
                 )
-            codes, scales = quantize("h%d" % first, h_grouped[:].rearrange("p j t -> p (j t)"), width)
+            if group == 0:
+                codes, scales = quantize("lead", lead_grouped[:].rearrange("p j t -> p (j t)"), N + width)
+                wo_codes, wo_scales = codes[:, 0:N], scales[:, 0:N]
+                codes, scales = codes[:, N : N + width], scales[:, N : N + width]
+            else:
+                codes, scales = quantize("h%d" % first, h_grouped[:].rearrange("p j t -> p (j t)"), width)
             result = held("result%d" % first, [P, N // P, width], F32)
             for c in range(N // P):
                 cols = slice(c * P, (c + 1) * P)
-                bank = bank_tile((4, 5, 6, 7, 3, 0, 1, 4, 5, 6)[2 * group + c], [P, width])
+                bank = bank_tile((4, 5, 6, 7, 3, 4, 5, 6)[2 * group + c], [P, width])
                 nc.tensor.matmul_mx(
                     out=bank[:], lhsT=wo_codes[:, cols].bitcast(FP8X4), lhsT_scale=wo_scales[:, cols],
                     rhs=codes[:].bitcast(FP8X4), rhs_scale=scales[:], start=True, stop=True,

@@ -40,7 +40,8 @@ REUSED = {
     "road_scales": 40 * KIB, "planes": 40 * KIB, "sensor_picked": 43 * KIB,
     "sensor_plane": 26 * KIB, "wg0_grouped0": 28 * KIB, "wg0_grouped1": 30 * KIB,
         "ws_grouped": 60 * KIB, "gated0": 60 * KIB,
-    "lead_grouped": 56 * KIB, "h_grouped256": 56 * KIB, "h_grouped0": 18 * KIB, "parked_sensor384": 16 * KIB,
+    "h_grouped768": 56 * KIB, "h_grouped256": 56 * KIB,
+    "h768_scales": 16 * KIB, "parked_sensor384": 16 * KIB + 256, "h_grouped0": 18 * KIB + 256,
     "wv_codes": 44 * KIB, "wg1_grouped2": 44 * KIB, "wg1_grouped3": 45 * KIB,
 }
 
@@ -321,8 +322,12 @@ def tile_list_traffic_gated_forecast_kernel(
                     rhs=codes[:].bitcast(FP8X4), rhs_scale=scales[:], start=True, stop=True,
                 )
                 column = bias[:, PACK + c : PACK + c + 1]
-                if group == len(OUT_GROUPS) - 1 and c == 1:
+                if group >= len(OUT_GROUPS) - 2 and c == 1:
                     nc.vector.tensor_scalar(result[:, c, :], bank[:], column, None, ALU.add)
                 else:
                     nc.scalar.activation(result[:, c, :], bank[:], ACT.Identity, bias=column)
-            nc.sync.dma_start(out=out_rows[:, :, first : first + width], in_=result[:])
+            if group < len(OUT_GROUPS) - 1:
+                nc.sync.dma_start(out=out_rows[:, :, first : first + width], in_=result[:])
+            else:
+                for c, queue in enumerate((nc.scalar, nc.sync)):
+                    queue.dma_start(out=out_rows[:, c, first : first + width], in_=result[:, c, :])

@@ -138,7 +138,7 @@ def tile_list_traffic_gated_forecast_kernel(
         )
         nc.vector.tensor_copy(out=staged[ROAD_ROW:P, 0:ROAD_WORDS], in_=packed_planes[ROAD_ROW:P, :])
         planes = held("planes", [P, 2, PLANE_WORDS], I32)
-        for quad in range(4):
+        for quad in (0, 2, 1, 3):
             first = ROAD_ROW + 8 * quad
             nc.sync.dma_start(out=planes[32 * quad : 32 * quad + 4], in_=staged[first : first + 8, :])
         road_second = load_words("road_second", tab_words[1], T)
@@ -186,7 +186,7 @@ def tile_list_traffic_gated_forecast_kernel(
                     nc.scalar.copy(out=parked[t][:], in_=value_banks[half, t][:])
         sensor_words = load_words("sensor_words", tab2_words[0], T2)
         sensor_plane = held("sensor_plane", [P, S // 4], I32)
-        for quad in range(4):
+        for quad in (0, 2, 1, 3):
             row = 32 * quad + SENSOR_ROW
             first = SENSOR_LOAD_ROW + 4 * quad
             nc.sync.dma_start(out=sensor_plane[row : row + 4, :], in_=sensor_picked[first : first + 4, :])
@@ -266,19 +266,21 @@ def tile_list_traffic_gated_forecast_kernel(
                 sensor[start] = picked[:, start - first : start - first + CHUNK]
 
         sensor_banks = {}
-        for half in (DIRECT, PARKED):
-            for inside in range(0, HALF, CHUNK):
-                start = half * HALF + inside
-                bank = bank_tile(start // CHUNK, [P, PACK, CHUNK])
-                for t in range(PACK):
-                    cols = slice(t * P, (t + 1) * P)
-                    nc.tensor.matmul_mx(
-                        out=bank[:, t, :], lhsT=ws_codes[:, cols].bitcast(FP8X4), lhsT_scale=ws_scales[:, cols],
-                        rhs=sensor[start].bitcast(FP8X4),
-                        rhs_scale=sensor_plane[:].bitcast(U8)[SENSOR_ROW:P, start : start + CHUNK],
-                        start=True, stop=True,
-                    )
-                sensor_banks[start] = bank
+
+        def sensor_product(start, index):
+            bank = bank_tile(index, [P, PACK, CHUNK])
+            for t in range(PACK):
+                cols = slice(t * P, (t + 1) * P)
+                nc.tensor.matmul_mx(
+                    out=bank[:, t, :], lhsT=ws_codes[:, cols].bitcast(FP8X4), lhsT_scale=ws_scales[:, cols],
+                    rhs=sensor[start].bitcast(FP8X4),
+                    rhs_scale=sensor_plane[:].bitcast(U8)[SENSOR_ROW:P, start : start + CHUNK],
+                    start=True, stop=True,
+                )
+            sensor_banks[start] = bank
+
+        for start in (512, 640, 768, 896, 384, 0):
+            sensor_product(start, start // CHUNK)
 
         lead_grouped = held("lead_grouped", [P, N + OUT_GROUPS[0][1], PACK], BF16)
         nc.scalar.copy(
@@ -316,7 +318,7 @@ def tile_list_traffic_gated_forecast_kernel(
             result = held("result%d" % first, [P, N // P, width], F32)
             for c in range(N // P):
                 cols = slice(c * P, (c + 1) * P)
-                bank = bank_tile((4, 5, 6, 7, 3, 4, 5, 6)[2 * group + c], [P, width])
+                bank = bank_tile((1, 2, 4, 5, 6, 3, 2, 4)[2 * group + c], [P, width])
                 nc.tensor.matmul_mx(
                     out=bank[:], lhsT=wo_codes[:, cols].bitcast(FP8X4), lhsT_scale=wo_scales[:, cols],
                     rhs=codes[:].bitcast(FP8X4), rhs_scale=scales[:], start=True, stop=True,
@@ -326,7 +328,10 @@ def tile_list_traffic_gated_forecast_kernel(
                     nc.vector.tensor_scalar(result[:, c, :], bank[:], column, None, ALU.add)
                 else:
                     nc.scalar.activation(result[:, c, :], bank[:], ACT.Identity, bias=column)
-            if group < len(OUT_GROUPS) - 1:
+            if group == 1:
+                sensor_product(128, 7)
+                sensor_product(256, 1)
+            if group < len(OUT_GROUPS) - 2:
                 nc.sync.dma_start(out=out_rows[:, :, first : first + width], in_=result[:])
             else:
                 for c, queue in enumerate((nc.scalar, nc.sync)):

@@ -38,11 +38,11 @@ REUSED = {
     "wg_first": 16 * KIB, "wo_raw": 16 * KIB, "packed_planes": 24 * KIB - 512,
     "road_second": 24 * KIB, "sensor_words": 32 * KIB,
     "road_scales": 40 * KIB, "planes": 40 * KIB, "sensor_picked": 43 * KIB,
-    "sensor_plane": 26 * KIB, "wg0_grouped0": 28 * KIB, "wg0_grouped1": 30 * KIB,
-        "ws_grouped": 60 * KIB, "gated0": 60 * KIB,
+    "sensor_plane": 26 * KIB, "wg0_grouped": 28 * KIB,
+        "ws_grouped": 60 * KIB, "gated0": 62 * KIB, "parked3": 59 * KIB,
     "h_grouped768": 56 * KIB, "h_grouped256": 56 * KIB,
     "h768_scales": 16 * KIB, "parked_sensor384": 16 * KIB + 256, "h_grouped0": 18 * KIB + 256,
-    "wv_codes": 44 * KIB, "wg1_grouped2": 44 * KIB, "wg1_grouped3": 45 * KIB,
+    "wv_codes": 44 * KIB, "wg1_grouped2": 44 * KIB, "late_pair": 45 * KIB,
 }
 
 
@@ -177,13 +177,17 @@ def tile_list_traffic_gated_forecast_kernel(
                 value_banks[half, t] = bank_tile(PACK * half + t, [P, HALF])
                 value_pass(value_banks[half, t], 0, half, t)
         parked = {}
+
+        def park_value(t):
+            parked[t] = held("parked%d" % t, [P, HALF], F32)
+            nc.scalar.copy(out=parked[t][:], in_=value_banks[PARKED, t][:])
+
         for half in (PARKED, DIRECT):
             road[1, half] = gather_half("road1_%d" % half, road_second, road_list, half)
             for t in range(PACK):
                 value_pass(value_banks[half, t], 1, half, t)
-                if half == PARKED:
-                    parked[t] = held("parked%d" % t, [P, HALF], F32)
-                    nc.scalar.copy(out=parked[t][:], in_=value_banks[half, t][:])
+                if half == PARKED and t < PACK - 1:
+                    park_value(t)
         sensor_words = load_words("sensor_words", tab2_words[0], T2)
         sensor_plane = held("sensor_plane", [P, S // 4], I32)
         for quad in (0, 2, 1, 3):
@@ -202,14 +206,19 @@ def tile_list_traffic_gated_forecast_kernel(
             )
 
         gate_banks = {}
-        pairs = [held("wg0_grouped%d" % u, [P, 2, P, PACK], BF16) for u in range(2)]
-        for t in range(PACK):
-            target, source = slot_views(pairs[t // 2][:, t % 2], wg_first, t)
+        last = PACK - 1
+        early = held("wg0_grouped", [P, last, P, PACK], BF16)
+        late_pair = held("late_pair", [P, 2, P, PACK], BF16)
+        for t in range(last):
+            target, source = slot_views(early[:, t], wg_first, t)
             nc.vector.tensor_copy(out=target, in_=source)
-        for u in range(2):
-            codes, scales = quantize("wg0_%d" % u, pairs[u][:].rearrange("p t m j -> p (t m j)"), 2 * P)
-            for e in range(2):
-                t = 2 * u + e
+        target, source = slot_views(late_pair[:, 0], wg_first, last)
+        nc.scalar.copy(out=target, in_=source)
+        for first, count in ((0, 2), (2, 1)):
+            grouped = early[:, first : first + count].rearrange("p t m j -> p (t m j)")
+            codes, scales = quantize("wg0_%d" % first, grouped, count * P)
+            for e in range(count):
+                t = first + e
                 wg_q[0, t] = (codes[:, e * P : (e + 1) * P], scales[:, e * P : (e + 1) * P])
                 gate_banks[DIRECT, t] = bank_tile(t, [P, HALF])
                 gate_pass(gate_banks[DIRECT, t], 0, DIRECT, t)
@@ -218,7 +227,7 @@ def tile_list_traffic_gated_forecast_kernel(
         for t in range(PACK):
             nc.sync.dma_start(out=wo_raw[:, t, :], in_=wo_rows[t])
 
-        slots = [held("wg1_grouped%d" % t, [P, P, PACK], BF16) for t in range(PACK)]
+        slots = [held("wg1_grouped%d" % t, [P, P, PACK], BF16) for t in range(last)] + [late_pair[:, 1]]
         for t in range(PACK):
             target, source = slot_views(slots[t][:], wg_second, t)
             if t < 2:
@@ -233,11 +242,18 @@ def tile_list_traffic_gated_forecast_kernel(
             nc.scalar.activation(gate[:], gate_banks[half, t][:], ACT.Sigmoid, bias=bias[:, t : t + 1])
             return gate
 
-        for t in range(PACK):
+        for t in range(last):
             codes, scales = quantize("wg1_%d" % t, slots[t][:].rearrange("p m j -> p (m j)"), P)
             wg_q[1, t] = (codes[:], scales[:])
             gate_pass(gate_banks[DIRECT, t], 1, DIRECT, t)
+        codes, scales = quantize("wg_last", late_pair[:].rearrange("p a m j -> p (a m j)"), 2 * P)
+        for a in range(2):
+            wg_q[a, last] = (codes[:, a * P : (a + 1) * P], scales[:, a * P : (a + 1) * P])
         for t in range(PACK):
+            if t == PACK - 1:
+                gate_banks[DIRECT, t] = bank_tile(0, [P, HALF])
+                for a in range(2):
+                    gate_pass(gate_banks[DIRECT, t], a, DIRECT, t)
             nc.vector.tensor_tensor(
                 gated[DIRECT][:, t, :], value_banks[DIRECT, t][:], sigmoid_gate(DIRECT, t)[:], ALU.mult
             )
@@ -253,10 +269,13 @@ def tile_list_traffic_gated_forecast_kernel(
         ws_codes, ws_scales = quantize("ws", ws_grouped[:].rearrange("p t m j -> p (t m j)"), H)
         gated[PARKED] = held("gated0", [P, PACK, HALF], F32)
         for t in range(PACK):
-            gate_banks[PARKED, t] = bank_tile(t, [P, HALF])
+            gate_banks[PARKED, t] = bank_tile((t + 1) % (PACK - 1), [P, HALF])
             for a in range(2):
                 gate_pass(gate_banks[PARKED, t], a, PARKED, t)
-            nc.gpsimd.tensor_tensor(gated[PARKED][:, t, :], parked[t][:], sigmoid_gate(PARKED, t)[:], ALU.mult)
+            gate = sigmoid_gate(PARKED, t)
+            if t == PACK - 1:
+                park_value(t)
+            nc.gpsimd.tensor_tensor(gated[PARKED][:, t, :], parked[t][:], gate[:], ALU.mult)
 
         sensor = {}
         for first, count in SENSOR_PIECES:
@@ -279,8 +298,9 @@ def tile_list_traffic_gated_forecast_kernel(
                 )
             sensor_banks[start] = bank
 
-        for start in (512, 640, 768, 896, 384, 0):
-            sensor_product(start, start // CHUNK)
+        for first, count in SENSOR_PIECES:
+            for start in range(first, first + count, CHUNK):
+                sensor_product(start, start // CHUNK)
 
         lead_grouped = held("lead_grouped", [P, N + OUT_GROUPS[0][1], PACK], BF16)
         nc.scalar.copy(
@@ -318,7 +338,7 @@ def tile_list_traffic_gated_forecast_kernel(
             result = held("result%d" % first, [P, N // P, width], F32)
             for c in range(N // P):
                 cols = slice(c * P, (c + 1) * P)
-                bank = bank_tile((1, 2, 4, 5, 6, 3, 2, 4)[2 * group + c], [P, width])
+                bank = bank_tile((4, 5, 6, 7, 3, 4, 5, 6)[2 * group + c], [P, width])
                 nc.tensor.matmul_mx(
                     out=bank[:], lhsT=wo_codes[:, cols].bitcast(FP8X4), lhsT_scale=wo_scales[:, cols],
                     rhs=codes[:].bitcast(FP8X4), rhs_scale=scales[:], start=True, stop=True,
@@ -328,9 +348,6 @@ def tile_list_traffic_gated_forecast_kernel(
                     nc.vector.tensor_scalar(result[:, c, :], bank[:], column, None, ALU.add)
                 else:
                     nc.scalar.activation(result[:, c, :], bank[:], ACT.Identity, bias=column)
-            if group == 1:
-                sensor_product(128, 7)
-                sensor_product(256, 1)
             if group < len(OUT_GROUPS) - 2:
                 nc.sync.dma_start(out=out_rows[:, :, first : first + width], in_=result[:])
             else:

from contextlib import ExitStack

import concourse.mybir as mybir

K, K2, H, N, T, T2, S = 1024, 512, 512, 256, 4096, 2048, 1024
FLOPS = 2 * S * (2 * K * H + K2 * H + H * N)

F32 = mybir.dt.float32
BF16 = mybir.dt.bfloat16
I32 = mybir.dt.int32
U32 = mybir.dt.uint32
U16 = mybir.dt.uint16
U8 = mybir.dt.uint8
FP8X4 = mybir.dt.float8_e4m3fn_x4
FP4X4 = mybir.dt.float4_e2m1fn_x4
ACT = mybir.ActivationFunctionType
ALU = mybir.AluOpType

P = 128
PACK = 4
K_PASS = P * PACK
HALF = 512
CHUNK = 128
PARKED, DIRECT = 0, 1
OUT_GROUPS = ((512, 256), (768, 256), (0, 256), (256, 256))
POOL_CHUNKS = (384,)
SENSOR_PIECES = ((512, 256), (768, 256), (0, 512))
LIST_COLS = S // 16
ROAD_ROW = P - 32
SENSOR_LOAD_ROW = P - 16
SENSOR_ROW = 8
BIAS_ROW = P - 6
ROAD_WORDS = S // 4
PLANE_WORDS = ROAD_WORDS + H // 4
KIB = 1024
REUSED = {
    "road_first": 0, "wg_second": 0, "ws_raw": 8 * KIB,
    "wg_first": 16 * KIB, "wo_raw": 16 * KIB, "packed_planes": 24 * KIB - 512,
    "road_second": 24 * KIB, "sensor_words": 32 * KIB,
    "road_scales": 40 * KIB, "planes": 40 * KIB, "sensor_picked": 43 * KIB,
    "sensor_plane": 26 * KIB, "wg0_grouped": 28 * KIB,
        "ws_grouped": 60 * KIB, "gated0": 62 * KIB, "parked3": 59 * KIB,
    "h_grouped768": 56 * KIB, "h_grouped256": 56 * KIB,
    "h768_scales": 16 * KIB, "parked_sensor384": 16 * KIB + 256, "h_grouped0": 18 * KIB + 256,
    "wv_codes": 44 * KIB, "wg1_grouped2": 44 * KIB, "late_pair": 45 * KIB,
}


def tile_list_traffic_gated_forecast_kernel(
    tc, tab_words, tab_scales, tab2_words, tab2_scales, offs, offs2,
    wg, bg, wv_words, wv_scales, ws, wo, bo, out,
):
    nc = tc.nc
    with ExitStack() as ctx:
        keep = ctx.enter_context(tc.tile_pool(name="keep", bufs=1))
        reused = ctx.enter_context(tc.tile_pool(name="reused", bufs=1))
        psum = ctx.enter_context(tc.psum_pool(name="psum", bufs=1))

        def bank_tile(index, shape):
            return psum.tile(shape, F32, name="bank%d" % index)

        def held(name, shape, dtype):
            if name in REUSED:
                return reused.tile(shape, dtype, name=name, align_bytes=64, offset=REUSED[name])
            return keep.tile(shape, dtype, name=name, align_bytes=64)

        def load_words(name, words, columns):
            table = held(name, [P, columns], I32)
            nc.sync.dma_start(out=table[:], in_=words.rearrange("p t i -> p (t i)").bitcast(I32))
            return table

        def load_weight(name, rows):
            raw = held(name, [P, PACK, H], F32)
            nc.sync.dma_start(out=raw[:], in_=rows.rearrange("(p j) c -> p j c", j=PACK))
            return raw

        def gather(name, window, offsets, count, dtype):
            picked = held(name, [P, count if dtype == U32 else count // 4], I32)
            nc.vector.tensor_copy(picked[:].bitcast(dtype), window[:].bitcast(dtype).indirect(offsets))
            return picked

        def gather_half(name, window, index_list, half):
            columns = LIST_COLS // 2
            return gather(name, window, index_list[:, half * columns : (half + 1) * columns], HALF, U32)

        def quantize(name, grouped, width):
            codes = held(name + "_codes", [P, width], U32)
            scales = held(name + "_scales", [P, width], U8)
            nc.vector.quantize_mx(out=codes[:].bitcast(FP8X4), scales=scales[:], in_=grouped)
            return codes, scales

        def slot_views(grouped, raw, t):
            source = raw[:].rearrange("p j (b t u i) -> p t b u j i", t=PACK, u=4, i=2)
            return grouped.rearrange("p (b u i) j -> p b u j i", u=4, i=2), source[:, t]

        road_list = keep.tile([P, LIST_COLS], U16, name="road_list")
        sensor_list = keep.tile([P, LIST_COLS], U16, name="sensor_list")
        road_scales = held("road_scales", [P, T // 4], I32)
        sensor_scales = held("sensor_scales", [P, T2 // 4], I32)
        wv_scale_rows = held("wv_scale_rows", [P, H // 4], I32)
        wv_raw = held("wv_raw", [P, 2, H // 2], I32)
        zeros = held("zeros", [P, P], F32)
        identity = held("identity", [P, P], F32)
        bias_rows = held("bias_rows", [P, P], F32)

        nc.sync.dma_start(road_list[:], offs)
        nc.sync.dma_start(out=road_scales[ROAD_ROW:P, :], in_=tab_scales.rearrange("a q t -> q a t").bitcast(I32))
        nc.sync.dma_start(out=wv_scale_rows[ROAD_ROW:P, :], in_=wv_scales.rearrange("a q n -> q a n").bitcast(I32))
        nc.sync.dma_start(sensor_list[:], offs2)
        nc.sync.dma_start(out=sensor_scales[SENSOR_LOAD_ROW:P, :], in_=tab2_scales[0].bitcast(I32))
        nc.sync.dma_start(out=wv_raw[:], in_=wv_words.rearrange("a p n -> p a n").bitcast(I32))
        road_first = load_words("road_first", tab_words[0], T)

        nc.vector.memset(zeros[:], 0.0)
        warm = held("warm", [P, 1], F32)
        nc.scalar.activation(warm[:], zeros[:, 0:1], ACT.Sigmoid)
        nc.vector.memset(road_scales[0:ROAD_ROW, :], 0)
        nc.vector.memset(sensor_scales[0:SENSOR_LOAD_ROW, :], 0)
        nc.vector.memset(bias_rows[0:BIAS_ROW, :], 0.0)
        nc.gpsimd.affine_select(
            out=identity[:], in_=zeros[:], pattern=[[-1, P]], compare_op=ALU.not_equal, fill=1.0,
            base=0, channel_multiplier=1,
        )
        nc.gpsimd.dma_start(
            out=bias_rows[BIAS_ROW : BIAS_ROW + PACK, :], in_=bg.rearrange("(b t q) -> t b q", t=PACK, q=8)
        )
        nc.gpsimd.dma_start(out=bias_rows[BIAS_ROW + PACK : P, :], in_=bo.rearrange("(c p) -> c p", p=P))
        bias = held("bias", [P, P - BIAS_ROW], F32)
        bias_bank = bank_tile(7, [P, P])
        nc.tensor.transpose(bias_bank[:], bias_rows[:], identity[:])
        nc.scalar.copy(out=bias[:], in_=bias_bank[:, BIAS_ROW:P])

        packed_planes = gather("packed_planes", road_scales, road_list[:], S, U8)
        staged = held("staged", [P, PLANE_WORDS], I32)
        nc.vector.tensor_copy(
            out=staged[ROAD_ROW:P, ROAD_WORDS:PLANE_WORDS].rearrange("p (t b w) -> p t b w", t=PACK, w=2),
            in_=wv_scale_rows[ROAD_ROW:P, :].rearrange("p (b t w) -> p t b w", t=PACK, w=2),
        )
        nc.vector.tensor_copy(out=staged[ROAD_ROW:P, 0:ROAD_WORDS], in_=packed_planes[ROAD_ROW:P, :])
        planes = held("planes", [P, 2, PLANE_WORDS], I32)
        for quad in (0, 2, 1, 3):
            first = ROAD_ROW + 8 * quad
            nc.sync.dma_start(out=planes[32 * quad : 32 * quad + 4], in_=staged[first : first + 8, :])
        road_second = load_words("road_second", tab_words[1], T)
        wg_first = load_weight("wg_first", wg[0:K_PASS, :])

        wv_codes = held("wv_codes", [P, 2, H // 2], I32)
        for a in range(2):
            nc.vector.tensor_copy(
                out=wv_codes[:, a, :].rearrange("p (t b w) -> p t b w", t=PACK, w=4),
                in_=wv_raw[:, a, :].rearrange("p (b t w) -> p t b w", t=PACK, w=4),
            )
        sensor_picked = gather("sensor_picked", sensor_scales, sensor_list[:], S, U8)

        road = {}
        for half in (PARKED, DIRECT):
            road[0, half] = gather_half("road0_%d" % half, road_first, road_list, half)
        wg_second = load_weight("wg_second", wg[K_PASS:K, :])
        ws_raw = load_weight("ws_raw", ws)

        def road_operand(a, half):
            cols = slice(half * HALF, (half + 1) * HALF)
            return road[a, half][:].bitcast(FP8X4), planes[:, a, 0:ROAD_WORDS].bitcast(U8)[:, cols]

        def value_pass(bank, a, half, t):
            rhs, rhs_scale = road_operand(a, half)
            nc.tensor.matmul_mx(
                out=bank[:],
                lhsT=wv_codes[:, a, :].bitcast(U8)[:, 2 * t * P : 2 * (t + 1) * P].bitcast(FP4X4),
                lhsT_scale=planes[:, a, ROAD_WORDS:PLANE_WORDS].bitcast(U8)[:, t * P : (t + 1) * P],
                rhs=rhs, rhs_scale=rhs_scale, start=(a == 0), stop=(a == 1),
            )

        value_banks = {}
        for half in (PARKED, DIRECT):
            for t in range(PACK):
                value_banks[half, t] = bank_tile(PACK * half + t, [P, HALF])
                value_pass(value_banks[half, t], 0, half, t)
        parked = {}

        def park_value(t):
            parked[t] = held("parked%d" % t, [P, HALF], F32)
            nc.scalar.copy(out=parked[t][:], in_=value_banks[PARKED, t][:])

        for half in (PARKED, DIRECT):
            road[1, half] = gather_half("road1_%d" % half, road_second, road_list, half)
            for t in range(PACK):
                value_pass(value_banks[half, t], 1, half, t)
                if half == PARKED and t < PACK - 1:
                    park_value(t)
        sensor_words = load_words("sensor_words", tab2_words[0], T2)
        sensor_plane = held("sensor_plane", [P, S // 4], I32)
        for quad in (0, 2, 1, 3):
            row = 32 * quad + SENSOR_ROW
            first = SENSOR_LOAD_ROW + 4 * quad
            nc.sync.dma_start(out=sensor_plane[row : row + 4, :], in_=sensor_picked[first : first + 4, :])

        wg_q = {}

        def gate_pass(bank, a, half, t):
            codes, scales = wg_q[a, t]
            rhs, rhs_scale = road_operand(a, half)
            nc.tensor.matmul_mx(
                out=bank[:], lhsT=codes.bitcast(FP8X4), lhsT_scale=scales,
                rhs=rhs, rhs_scale=rhs_scale, start=(a == 0), stop=(a == 1),
            )

        gate_banks = {}
        last = PACK - 1
        early = held("wg0_grouped", [P, last, P, PACK], BF16)
        late_pair = held("late_pair", [P, 2, P, PACK], BF16)
        for t in range(last):
            target, source = slot_views(early[:, t], wg_first, t)
            nc.vector.tensor_copy(out=target, in_=source)
        target, source = slot_views(late_pair[:, 0], wg_first, last)
        nc.scalar.copy(out=target, in_=source)
        for first, count in ((0, 2), (2, 1)):
            grouped = early[:, first : first + count].rearrange("p t m j -> p (t m j)")
            codes, scales = quantize("wg0_%d" % first, grouped, count * P)
            for e in range(count):
                t = first + e
                wg_q[0, t] = (codes[:, e * P : (e + 1) * P], scales[:, e * P : (e + 1) * P])
                gate_banks[DIRECT, t] = bank_tile(t, [P, HALF])
                gate_pass(gate_banks[DIRECT, t], 0, DIRECT, t)
        wo_raw = held("wo_raw", [P, PACK, N], F32)
        wo_rows = wo.rearrange("(b t q) n -> t b q n", t=PACK, q=8)
        for t in range(PACK):
            nc.sync.dma_start(out=wo_raw[:, t, :], in_=wo_rows[t])

        slots = [held("wg1_grouped%d" % t, [P, P, PACK], BF16) for t in range(last)] + [late_pair[:, 1]]
        for t in range(PACK):
            target, source = slot_views(slots[t][:], wg_second, t)
            if t < 2:
                nc.vector.tensor_copy(out=target, in_=source)
            else:
                nc.scalar.copy(out=target, in_=source)

        gated = {DIRECT: held("gated1", [P, PACK, HALF], F32)}

        def sigmoid_gate(half, t):
            gate = held("gate%d_%d" % (half, t), [P, HALF], F32)
            nc.scalar.activation(gate[:], gate_banks[half, t][:], ACT.Sigmoid, bias=bias[:, t : t + 1])
            return gate

        for t in range(last):
            codes, scales = quantize("wg1_%d" % t, slots[t][:].rearrange("p m j -> p (m j)"), P)
            wg_q[1, t] = (codes[:], scales[:])
            gate_pass(gate_banks[DIRECT, t], 1, DIRECT, t)
        codes, scales = quantize("wg_last", late_pair[:].rearrange("p a m j -> p (a m j)"), 2 * P)
        for a in range(2):
            wg_q[a, last] = (codes[:, a * P : (a + 1) * P], scales[:, a * P : (a + 1) * P])
        for t in range(PACK):
            if t == PACK - 1:
                gate_banks[DIRECT, t] = bank_tile(0, [P, HALF])
                for a in range(2):
                    gate_pass(gate_banks[DIRECT, t], a, DIRECT, t)
            nc.vector.tensor_tensor(
                gated[DIRECT][:, t, :], value_banks[DIRECT, t][:], sigmoid_gate(DIRECT, t)[:], ALU.mult
            )

        ws_grouped = held("ws_grouped", [P, PACK, P, PACK], BF16)
        nc.gpsimd.tensor_scalar(
            ws_grouped[:, 0 : PACK - 1].rearrange("p t (b q) j -> p b t (q j)", q=8),
            ws_raw[:].rearrange("p j (b c) -> p b c j", c=32)[:, :, 0 : 8 * (PACK - 1), :],
            1.0, 0.0, ALU.mult, ALU.add,
        )
        target, source = slot_views(ws_grouped[:, PACK - 1], ws_raw, PACK - 1)
        nc.scalar.copy(out=target, in_=source)
        ws_codes, ws_scales = quantize("ws", ws_grouped[:].rearrange("p t m j -> p (t m j)"), H)
        gated[PARKED] = held("gated0", [P, PACK, HALF], F32)
        for t in range(PACK):
            gate_banks[PARKED, t] = bank_tile((t + 1) % (PACK - 1), [P, HALF])
            for a in range(2):
                gate_pass(gate_banks[PARKED, t], a, PARKED, t)
            gate = sigmoid_gate(PARKED, t)
            if t == PACK - 1:
                park_value(t)
            nc.gpsimd.tensor_tensor(gated[PARKED][:, t, :], parked[t][:], gate[:], ALU.mult)

        sensor = {}
        for first, count in SENSOR_PIECES:
            offsets = sensor_list[:, first // 16 : (first + count) // 16]
            picked = gather("sensor%d" % first, sensor_words, offsets, count, U32)
            for start in range(first, first + count, CHUNK):
                sensor[start] = picked[:, start - first : start - first + CHUNK]

        sensor_banks = {}

        def sensor_product(start, index):
            bank = bank_tile(index, [P, PACK, CHUNK])
            for t in range(PACK):
                cols = slice(t * P, (t + 1) * P)
                nc.tensor.matmul_mx(
                    out=bank[:, t, :], lhsT=ws_codes[:, cols].bitcast(FP8X4), lhsT_scale=ws_scales[:, cols],
                    rhs=sensor[start].bitcast(FP8X4),
                    rhs_scale=sensor_plane[:].bitcast(U8)[SENSOR_ROW:P, start : start + CHUNK],
                    start=True, stop=True,
                )
            sensor_banks[start] = bank

        for first, count in SENSOR_PIECES:
            for start in range(first, first + count, CHUNK):
                sensor_product(start, start // CHUNK)

        lead_grouped = held("lead_grouped", [P, N + OUT_GROUPS[0][1], PACK], BF16)
        nc.scalar.copy(
            out=lead_grouped[:, 0:N, :].rearrange("p (c i) t -> p c t i", i=2),
            in_=wo_raw[:].rearrange("p t (c i) -> p c t i", i=2),
        )

        out_rows = out.rearrange("(c p) j -> p c j", p=P)
        for group, (first, width) in enumerate(OUT_GROUPS):
            if group == 0:
                h_grouped = lead_grouped[:, N : N + width, :]
            else:
                h_grouped = held("h_grouped%d" % first, [P, width, PACK], BF16)
            for start in range(first, first + width, CHUNK):
                half, inside = divmod(start, HALF)
                bank = sensor_banks[start]
                h_part = h_grouped[:, start - first : start - first + CHUNK, :]
                engine = nc.vector
                if start in POOL_CHUNKS:
                    parked_sensor = held("parked_sensor%d" % start, [P, PACK, CHUNK], F32)
                    nc.scalar.copy(out=parked_sensor[:], in_=bank[:])
                    bank, engine = parked_sensor, nc.gpsimd
                engine.tensor_tensor(
                    h_part.rearrange("p (c i) t -> p c t i", i=2),
                    bank[:].rearrange("p t (c i) -> p c t i", i=2),
                    gated[half][:, :, inside : inside + CHUNK].rearrange("p t (c i) -> p c t i", i=2),
                    ALU.add,
                )
            if group == 0:
                codes, scales = quantize("lead", lead_grouped[:].rearrange("p j t -> p (j t)"), N + width)
                wo_codes, wo_scales = codes[:, 0:N], scales[:, 0:N]
                codes, scales = codes[:, N : N + width], scales[:, N : N + width]
            else:
                codes, scales = quantize("h%d" % first, h_grouped[:].rearrange("p j t -> p (j t)"), width)
            result = held("result%d" % first, [P, N // P, width], F32)
            for c in range(N // P):
                cols = slice(c * P, (c + 1) * P)
                bank = bank_tile((4, 5, 6, 7, 3, 4, 5, 6)[2 * group + c], [P, width])
                nc.tensor.matmul_mx(
                    out=bank[:], lhsT=wo_codes[:, cols].bitcast(FP8X4), lhsT_scale=wo_scales[:, cols],
                    rhs=codes[:].bitcast(FP8X4), rhs_scale=scales[:], start=True, stop=True,
                )
                column = bias[:, PACK + c : PACK + c + 1]
                if group >= len(OUT_GROUPS) - 2 and c == 1:
                    nc.vector.tensor_scalar(result[:, c, :], bank[:], column, None, ALU.add)
                else:
                    nc.scalar.activation(result[:, c, :], bank[:], ACT.Identity, bias=column)
            if group < len(OUT_GROUPS) - 2:
                nc.sync.dma_start(out=out_rows[:, :, first : first + width], in_=result[:])
            else:
                for c, queue in enumerate((nc.scalar, nc.sync)):
                    queue.dma_start(out=out_rows[:, c, first : first + width], in_=result[:, c, :])
